import numpy as np, ml_dtypes
CORES = [16,18,20,22]
N = 4
BF = ml_dtypes.bfloat16
W, E, B, C, RO, NC = 1024, 2048, 256, 11, 3, 32
def group(rng, noise, good, mode, proto):
    n = W // NC; mem = rng.permutation(W).reshape(NC, n); cl = np.zeros(W, np.int64); cl[mem] = np.arange(NC)[:, None]
    x = np.minimum(np.maximum(proto[:, cl] + rng.integers(-noise, noise + 1, (16, W)), 0), 63)
    nx = rng.integers(0, NC, (16, NC))
    if mode == 1: nx[:] = np.arange(NC)
    if mode == 2: nx[:] = cl[0]
    if mode == 3: nx[:] = cl[W - 1]
    l = mem[nx[:, cl], rng.integers(0, n, (16, W))]
    if mode == 1: l[:] = np.arange(W)
    if mode == 2: l[:] = 0
    if mode == 3: l[:] = W - 1
    i = np.zeros((16, E), np.int64); q = rng.integers(0, NC, E)
    for k in range(16):
        i[k] = mem[q, rng.integers(0, n, E)]
        if k < 15:
            go = nx[k, q]; q = np.where(good[k], go, (go + rng.integers(1, NC, E)) % NC)
    return x, i, l
def parts(rng, style):
    x = np.zeros((N, 8, 16, W), np.int64); i = np.zeros((N, 8, 16, E), np.int64); l = np.zeros((N, 8, 16, W), np.int64)
    for a in range(N):
        for g in range(8):
            noise = int(rng.integers(1, 4)); mode = 0; proto = rng.integers(0, 64, (16, NC))
            good = rng.random((15, E)) < rng.choice(np.array([0.2, 0.6, 0.8, 0.95, 1.0]), E)
            if style == "ties": noise = 0; proto = 16 + 8 * rng.integers(0, 2, (16, NC))
            if style == "corners":
                noise = 0; mode = (a + g) % 4; n = rng.choice(np.array([0, 1, C - 1, C, C + 1, 15]), E)
                good = np.argsort(np.argsort(rng.random((15, E)), axis=0), axis=0) < n
            x[a, g], i[a, g], l[a, g] = group(rng, noise, good, mode, proto)
    t = np.stack([rng.integers(20, 70, (N, 8, 16)), rng.integers(200, 420, (N, 8, 16))], axis=-1)
    return x, rng.integers(0, 64, (N, 8, 16, E)), i, l, rng.integers(0, 64, (N, 8, 16, B)), rng.integers(0, 256, (N, 8, 16, 1)), rng.integers(0, 2048, (N, 8, 16, 2)), t
def pack(x, gs, i, l, z, w, h, t):
    def bf(v): return np.ascontiguousarray(v.reshape(N, 128, -1)).astype(np.float32).astype(BF)
    def whole(v): return np.ascontiguousarray(v.reshape(N, 128, -1)).astype(np.int32)
    return {"xc": bf(x), "gi": bf(gs), "ix": whole(i), "lk": whole(l), "zc": bf(z), "wt": whole(w), "hk": whole(h), "th": whole(t)}
def ends(rng, lo, hi, shape, share):
    v = np.where(rng.random(shape) < 0.5, lo, hi)
    return np.where(rng.random(shape) < share, v, rng.integers(lo, hi + 1, shape))
def records(rng, n):
    k = rng.integers(0, 3, (N, 8, 1, n))
    return np.where(k == 0, 0, np.where(k == 1, 63, ends(rng, 0, 63, (N, 8, 16, n), 1.0)))
def full(rng, p):
    u = rng.permutation(4096); f, k = np.unique(((u * u >> 5) + p * u) & (E - 1), return_index=True)
    return u[rng.permutation(k)[:B]]
def setup_inputs(rng):
    return pack(*parts(rng, "plain"))
def setup_inputs_ties(rng):
    x, gs, i, l, z, w, h, t = parts(rng, "ties")
    gs = 16 + 8 * rng.integers(0, 2, gs.shape); z = 16 + 8 * rng.integers(0, 2, z.shape)
    t = rng.choice(np.array([56, 63, 64, 65, 72]), t.shape)
    for a in range(N):
        for g in (6, 7):
            v = (256, 257, 259, 513, 515, 767, 1005, 1007)[(a + g) & 7]; base = int(rng.integers(0, 1008 - v))
            m = rng.permutation(W); low = np.flatnonzero(m < W // 2); high = np.flatnonzero(m >= W // 2)
            size = base + np.where(m < W // 2, 0, v + (rng.random(W) < 0.3).astype(np.int64))
            x[a, g] = (size >> 4) + (np.arange(16)[:, None] < (size & 15)).astype(np.int64)
            i[a, g] = low[rng.integers(0, W // 2, (16, E))]; l[a, g] = high[rng.integers(0, W // 2, (16, W))]
            t[a, g, :, 0] = v; t[a, g, :, 1] = 1008
    return pack(x, gs, i, l, z, w, h, t)
def setup_inputs_corners(rng):
    x, gs, i, l, z, w, h, t = parts(rng, "corners")
    for a in range(N):
        for g in range(8):
            kind = (3 * a + g) % 4
            if kind == 0: w[a, g] = 255
            if kind == 1: w[a, g] = 255 * rng.integers(0, 2, (16, 1))
            if kind == 2: w[a, g] = 0; w[a, g, 15] = 1
            t[a, g, :, 0] = (0, 1, 40, 0, 0, 1008, 40, 1)[(a + g) % 8]
            t[a, g, :, 1] = rng.choice(np.array([0, 340, 1008]), 16)
            h[a, g] = np.where(rng.random((16, 2)) < 0.4, 2047 * rng.integers(0, 2, (16, 2)), h[a, g])
    k = rng.integers(0, 4, (N, 8, 1, B)); z = np.where(k == 0, 0, np.where(k == 1, 63, z))
    k = rng.integers(0, 4, (N, 8, 1, E)); gs = np.where(k == 0, 0, np.where(k == 1, 63, gs))
    i = np.where(rng.random((N, 8, 1, E)) < 0.1, (W - 1) * rng.integers(0, 2, (N, 8, 1, E)), i)
    return pack(x, gs, i, l, z, w, h, t)
def setup_inputs_crowd(rng):
    x, gs, i, l, z, w, h, t = parts(rng, "plain")
    w[:, 0::4] = 0; w[:, 0::4, 5] = 1; z[:, 0::4, 5] = rng.integers(0, 6, (N, 2, B)); h[:, 0::4, :, 0] = 0
    i[:, 1] = rng.choice(np.array([0, 1, W // 2, W - 2, W - 1]), (N, 16, E)); gs[:, 1] = 30
    w[:, 2] = 0
    z[:, 3] = z[:, 3][..., rng.integers(0, 3, B)]
    for a in range(N):
        for g in (5, 6, 7):
            w[a, g] = 0; w[a, g, 0] = 1; w[a, g, 1] = 64; gs[a, g] = 0
            p = int(h[a, g, 0, 0]); u = full(rng, p)
            if g == 5: u[B // 2:] = u[:B // 2]
            z[a, g, 0] = u & 63; z[a, g, 1] = u >> 6
            e = ((u * u >> 5) + p * u) & (E - 1)
            if g == 5:
                side = rng.random(B // 2) < 0.5; side[0] = True; side[1] = False; near = np.concatenate([side, ~side])
                x[a, g] = rng.integers(16, 25, (16, W)); i[a, g] = rng.integers(0, W, (16, E))
                z[a, g, 2:] = np.where(near, rng.integers(16, 25, (14, B)), rng.integers(56, 64, (14, B)))
                t[a, g, :, 0] = 0; t[a, g, :, 1] = rng.integers(206, 448, 16)
            if g == 6:
                o = rng.permutation(W); i[a, g][:, e] = o[(np.arange(16)[:, None] % (W // B)) * B + np.arange(B)]
                t[a, g, :, 0] = 0
            if g == 7: t[a, g, :, 0] = 1008
    t[2, :, :, 0] = 0
    gs[2, 3] = 30; c = int(rng.integers(0, W)); u = np.add.reduce(w[2, 3] * z[2, 3], axis=0) & 4095
    e = ((u * u >> 5) + h[2, 3, 0, 0] * u) & (E - 1)
    i[2, 3][:, e] = c; l[2, 3][:, c] = c
    return pack(x, gs, i, l, z, w, h, t)
def setup_inputs_spread(rng):
    x, gs, i, l, z, w, h, t = parts(rng, "plain")
    x = x >> rng.integers(0, 7, (N, 8, 1, W)); gs = gs >> rng.integers(0, 7, (N, 8, 1, E)); z = z >> rng.integers(0, 7, (N, 8, 1, B))
    i[:, ::2] = (W * rng.random((N, 4, 16, E)) ** 3).astype(np.int64); l[:, ::4] = (W * rng.random((N, 2, 16, W)) ** 3).astype(np.int64)
    w = np.exp2(8 * rng.random(w.shape)).astype(np.int64); h = np.exp2(11 * rng.random(h.shape)).astype(np.int64)
    t = np.minimum(np.exp2(10.2 * rng.random(t.shape)).astype(np.int64), 1008)
    return pack(x, gs, i, l, z, np.minimum(w, 255), np.minimum(h, 2047), t)
def setup_inputs_ends(rng):
    x = records(rng, W); gs = records(rng, E); z = records(rng, B)
    x[:, 0::2, :, 0] = 63; x[:, 0::2, :, W - 1] = 0; x[:, 1::2, :, 0] = 0; x[:, 1::2, :, W - 1] = 63
    i = ends(rng, 0, W - 1, (N, 8, 16, E), 0.75); l = ends(rng, 0, W - 1, (N, 8, 16, W), 0.75)
    w = ends(rng, 0, 255, (N, 8, 16, 1), 0.75); w[:, 7] = 255
    h = ends(rng, 0, 2047, (N, 8, 16, 2), 0.8); t = ends(rng, 0, 1008, (N, 8, 16, 2), 1.0)
    t[0, :, :, 0] = 1008; a = N - 1; t[a, 7, :, 0] = 0
    i[0, 5] = W - 1; l[0, 5, :, W - 1] = 0
    t[1, :, :, 0] = 1008; t[1, 6, :, 0] = 0
    w[1, 6] = 0; w[1, 6, 15] = 255; z[1, 6, 15] = 0; z[1, 6, 15, B - 1] = 63; h[1, 6, :, 0] = 2047 * rng.integers(0, 2, 16)
    i[1, 6] = W - 1; i[1, 6, :, 0] = 0; l[1, 6, :, 0] = 0; l[1, 6, :, W - 1] = 0
    v = z[a, 7]; v[:, B - 1] = 63; v[:, B - 2] = 0; v[15, B - 2] = 63; v[:, B - 3] = 0; v[:4, B - 3] = 63; v[4, B - 3] = 5
    h[a, 7, 0, 0] = 2047; h[a, 7, 1, 0] = 0; h[a, 7, 15, 1] = 2047
    h[a, 7, 15, 0] = ((E - 1 - (3777 * 3777 >> 5)) * pow(3777, -1, E)) % E
    c = ((3088 * 3088 >> 5) + h[a, 7, :, 0] * 3088) & (E - 1)
    gs[a, 7][:, c] = 0; gs[a, 7, :, E - 1] = v[:, B - 2]
    i[a, 7, :, c[1]] = 0; i[a, 7, :, c[0]] = W - 1; i[a, 7, :8, E - 1] = 0; i[a, 7, 8:, E - 1] = W - 1
    l[a, 7, :, 0] = 0; l[a, 7, :, W - 1] = 0
    return pack(x, gs, i, l, z, w, h, t)
def check_inputs(d):
    bad = []
    for k, lo, hi in (("xc", 0, 63), ("gi", 0, 63), ("ix", 0, W - 1), ("lk", 0, W - 1), ("zc", 0, 63), ("wt", 0, 255), ("hk", 0, 2047), ("th", 0, 1008)):
        v = np.asarray(d[k]).astype(np.float64)
        if not np.all((v >= lo) & (v <= hi) & (v == np.floor(v))): bad.append("range of " + k)
    return bad
def reference(xc, gi, ix, lk, zc, wt, hk, th):
    def cut(v): return np.asarray(v).astype(np.float32).astype(np.int64).reshape(N, 8, 16, -1)
    X, G, I, L, Z, w, h, t = cut(xc), cut(gi), cut(ix), cut(lk), cut(zc), cut(wt), cut(hk), cut(th)
    A = np.zeros(N, np.int64); lane = np.arange(B)
    for rnd in range(RO):
        count = np.zeros(N, np.int64)
        for a in range(N):
            r = (a - rnd) % N
            for g in range(8):
                z = Z[r, g]
                u = np.add.reduce(w[a, g] * z, axis=0) & 4095
                em = ((u * u >> 5) + h[a, g, :, 0:1] * u + A[a]) & (E - 1)
                d = np.add.reduce(np.abs(G[a, g][:, em] - z[:, None, :]), axis=0)
                e = em[np.argmin(d, axis=0), lane]
                J = I[a, g][:, e]
                x = X[a, g][:, J]
                y = X[a, g][:, np.take_along_axis(L[a, g], J, 1)]
                s = np.add.reduce(np.abs(y[:, :15] - x[:, 1:]), axis=0)
                far = np.add.reduce(np.abs(x - z[:, None, :]), axis=0)
                rec = np.add.reduce((s <= t[a, g, :15, 0:1]).astype(np.int64), axis=0) >= C
                fresh = ((u * u >> 4) + h[a, g, :, 1:2] * u) & (W - 1)
                col = np.where(rec[None, :] | (far > t[a, g, :, 1:2]), fresh, J)
                ks = np.argmax(s, axis=0)
                f, first = np.unique(e, return_index=True)
                I[a, g][:, f] = col[:, first]
                if rnd < RO - 1:
                    o = first[rec[first]]; G[a, g][:, e[o]] = z[:, o]
                q = np.flatnonzero(~rec); c, one = np.unique(J[ks[q], q], return_index=True); q = q[one]
                L[a, g][ks[q], c] = J[ks[q] + 1, q]
                count[a] += np.count_nonzero(rec)
                Z[r, g] = (z + np.maximum.reduce(x, axis=1)) >> 1
        A = count
    return {"yz": Z.reshape(N, 128, B).astype(np.float32).astype(BF), "yi": I.reshape(N, 128, E).astype(np.float32), "yl": L.reshape(N, 128, W).astype(np.float32)}

@@ -1,0 +1,617 @@
+import numpy as np
+from concourse.mybir import AluOpType as OP, ActivationFunctionType as AF, AxisListType as AX
+
+W, E, B, RO, NEED = 1024, 2048, 256, 3, 11
+NENG = 4
+GPLAN = ("VSVS", "SSSV", "SSSV")
+YPLAN = ("SSSV", "SSSV", "SSSV")
+ZPLAN = ("VSVS", "VSVS", "VSVS")
+FPLAN = "SS"
+TRIES, ORDER = 500, {}
+HEAD, HZ, HC, LOOK = 5.0, 8.0, 8.0, 0.05
+F32, BF, F16, I32, U16 = "float32", "bfloat16", "float16", "int32", "uint16"
+
+SCRATCH = {
+    "gist": ("sbuf", [128, E + B], BF), "nm": ("sbuf", [128, E + B], F32), "lkt": ("sbuf", [128, W + B], F32),
+    "xcb": ("sbuf", [128, W], BF), "ixi": ("sbuf", [128, E], I32), "lki": ("sbuf", [128, W], I32),
+    "wti": ("sbuf", [128, 1], I32), "hki": ("sbuf", [128, 2], I32), "thi": ("sbuf", [128, 2], I32),
+    "zin0": ("sbuf", [128, B], BF), "zin1": ("sbuf", [128, B], BF), "zin2": ("sbuf", [128, B], BF), "zfin": ("sbuf", [128, B], BF),
+    "zo0": ("sbuf", [128, B], BF), "zo1": ("sbuf", [128, B], BF), "zo2": ("sbuf", [128, B], BF),
+    "S": ("sbuf", [128, 2048], BF), "SF": ("sbuf", [128, 2048], F16), "SW": ("sbuf", [128, 2048], BF), "D": ("sbuf", [128, 2048], F16), "R": ("sbuf", [128, 2048], F16),
+    "NS": ("sbuf", [128, 2048], BF), "rz": ("sbuf", [128, 2048], BF), "zr0": ("sbuf", [128, 4096], BF), "zr1": ("sbuf", [128, 4096], BF),
+    "eq": ("sbuf", [128, 16, 256], BF), "eq2": ("sbuf", [128, 16, 256], BF),
+}
+for _k in (0, 1):
+    for _n, _d, _w in (("gd", BF, 2048), ("fa", BF, 2048), ("nx", BF, 2064), ("lg", F16, 2048), ("yb", BF, 2048), ("zs", BF, 2048)):
+        SCRATCH["%s%d" % (_n, _k)] = ("sbuf", [128, _w], _d)
+    SCRATCH["aa%d" % _k] = ("sbuf", [128, 8, 16, 16], BF)
+    SCRATCH["ya%d" % _k] = ("sbuf", [128, 8, 16, 16], BF)
+_SMALL = {
+    F32: (("wtf", 1), ("hkf", 2), ("thf", 2), ("one", 128), ("idf", 128), ("blk", 128), ("wblk", 128), ("zer", 128), ("pm64", 64), ("pm32", 32), ("pm", 16), ("im", 16),
+          ("half", 16), ("zero", 16), ("pw", 16), ("tw", 16), ("tr", 16), ("wcol", 1), ("rcol", 1), ("kcol", 1), ("thr", 256), ("lane", 32), ("lan0", 16),
+          ("pd", 32), ("akey", 128), ("rmin", 128), ("rmax", 128), ("xe", 256), ("xq", 256), ("e0", 256), ("km0", 128), ("km1", 128), ("elf", 16),
+          ("ja", 256), ("kx0", 128), ("kx1", 128), ("rec", 16), ("nrec", 16), ("acol", 1), ("loL", 16), ("dE", 32), ("dT", 64), ("oT", 64), ("gT", 16),
+          ("IL", 16), ("dl", 256), ("nl", 256), ("pn", 256)),
+    F16: (("id16", 128), ("ni16", 128), ("hi16", 128), ("nh16", 128), ("sh16", 128), ("bo16", 128), ("nb16", 128), ("one16", 256), ("r0k", 128), ("prow", 128), ("imr", 128), ("c8k", 128),
+          ("ksr", 128), ("cf", 48), ("v160", 256), ("v161", 256), ("elh", 16), ("jh", 256), ("nh", 256), ("jr", 16), ("eB", 256), ("IB", 256), ("lo", 512),
+          ("oh", 256), ("pj", 256)),
+    BF: (("idb", 128), ("nib", 128), ("k1b", 128), ("oneb", 128), ("wd", 128), ("bo4", 128), ("rcnt", 128), ("ze", 256), ("cm0", 128), ("cm1", 128), ("cn0", 128), ("cn1", 128),
+         ("recb", 16), ("rB", 256), ("mk", 256)),
+    I32: (("ui", 32), ("sq", 16), ("cmb0", 48), ("cmb1", 48), ("bs", 16), ("ei", 256), ("ej", 256), ("vi", 256), ("vj", 256), ("ki", 64), ("el", 16), ("kj", 32)),
+    U16: (("e16", 256), ("elu", 16), ("ju", 256), ("nu", 256), ("of", 64), ("ILu", 16)),
+}
+PLACE = {}
+for _d, _a in ((F32, "fA"), (F16, "hA"), (BF, "bA"), (I32, "iA"), (U16, "uA")):
+    _at = 0
+    for _n, _w in _SMALL[_d]:
+        PLACE[_n] = (_a, _at, _w)
+        _at += -(-_w // 32) * 32
+    SCRATCH[_a] = ("sbuf", [128, _at], _d)
+for _k in range(8):
+    SCRATCH["ps%d" % _k] = ("psum", [128, 512], F32)
+NDMA = 20
+SEMAPHORES = ["eV", "eS", "eP", "eG", "snd", "arr1", "arr2", "arr3"] + ["d%d" % k for k in range(NDMA)]
+
+CY = 0.00083 * 1.25
+GA, SC, PEC = 1.56, 3.8, 0.0006
+
+
+def rank_program(g, core, T, topo):
+    rank = T.rank_of(core)
+    if rank is None:
+        return
+    ops, hist, head = [], {}, [0.0]
+    queues = {"V": g.vector, "S": g.scalar, "P": g.tensor, "G": g, "Y": g.sync}
+
+    def A(name, lo=0, hi=None, step=1):
+        if name in PLACE:
+            name, at, w = PLACE[name]
+            lo, hi = at + lo, at + (w if hi is None else hi)
+        hi = T[name].shape[1] if hi is None else hi
+        return (T[name][:, lo:hi] if step == 1 else T[name][:, lo:hi:step], (name, lo, hi, step))
+
+    def meets(a, b):
+        if a[1] >= b[2] or b[1] >= a[2]:
+            return False
+        return not (a[3] == b[3] and a[3] > 1 and a[1] % a[3] != b[1] % b[3])
+
+    def add(q, calls, w, r, cost, lat=0.0, kind="c", sem=None, val=1):
+        o = {"q": q, "calls": calls, "cost": cost, "lat": lat, "kind": kind, "sem": sem, "val": val, "deps": {}, "i": len(ops), "head": head[0]}
+        for regs, isw in ((r, False), (w, True)):
+            for reg in regs:
+                ps = reg[0][:2] == "ps"
+                for (p, preg, pw) in hist.setdefault(reg[0], []):
+                    same = p["q"] == q and p["kind"] == "c" and kind == "c"
+                    if ps and not same:
+                        o["deps"][p["i"]] = True
+                    elif meets(reg, preg) and (isw or pw):
+                        need = not (same and q == "P")
+                        o["deps"][p["i"]] = o["deps"].get(p["i"], False) or need
+        for regs, isw in ((r, False), (w, True)):
+            for reg in regs:
+                h = hist[reg[0]]
+                if isw and reg[3] == 1 and reg[0][:2] != "ps":
+                    h[:] = [x for x in h if not (x[0] is not o and x[1][1] >= reg[1] and x[1][2] <= reg[2])]
+                h.append((o, reg, isw))
+        ops.append(o)
+
+    def vcost(n, f=1.0):
+        return 0.06 + max(64.0, n * f) * CY
+
+    def width(x):
+        return (x[1][2] - x[1][1] + x[1][3] - 1) // x[1][3]
+
+    def fast(*xs):
+        return 0.5 if all(SCRATCH[x[1][0]][2] in (BF, F16, U16) for x in xs) else 1.0
+
+    def cp(o, i):
+        add("V", [lambda: g.vector.tensor_copy(o[0], i[0])], [o[1]], [i[1]], vcost(width(i), fast(o, i)))
+
+    def tt(o, a, b, op):
+        f = 1.0 if a[1][0][:2] == "ps" or b[1][0][:2] == "ps" else 2.0
+        add("V", [lambda: g.vector.tensor_tensor(o[0], a[0], b[0], op)], [o[1]], [a[1], b[1]], vcost(width(a), f))
+
+    def ts(o, a, s1, op0, s2=None, op1=None):
+        r = [a[1]] + [s[1] for s in (s1, s2) if isinstance(s, tuple)]
+        x1 = s1[0] if isinstance(s1, tuple) else s1
+        x2 = s2[0] if isinstance(s2, tuple) else s2
+        if op1 is None:
+            f = lambda: g.vector.tensor_scalar(o[0], a[0], x1, None, op0)
+        else:
+            f = lambda: g.vector.tensor_scalar(o[0], a[0], x1, x2, op0, op1)
+        add("V", [f], [o[1]], r, vcost(width(a), fast(o, a)))
+
+    def ms(o, v):
+        add("V", [lambda: g.vector.memset(o[0], v)], [o[1]], [], vcost(width(o), fast(o)))
+
+    def scan(o, d0, d1, init, op0, op1):
+        add("V", [lambda: g.vector.tensor_tensor_scan(o[0], d0[0], d1[0], init, op0, op1)], [o[1]], [d0[1], d1[1]], vcost(width(d1), fast(o, d0, d1)))
+
+    def total_of(o, i):
+        add("V", [lambda: g.vector.tensor_reduce(o[0], i[0], AX.X, OP.add)], [o[1]], [i[1]], vcost(width(i)))
+
+    def act(o, i, func, scale=1.0, bias=0.0):
+        r = [i[1]] + ([scale[1]] if isinstance(scale, tuple) else [])
+        sc = scale[0] if isinstance(scale, tuple) else scale
+        add("S", [lambda: g.scalar.activation(o[0], i[0], func, bias, sc)], [o[1]], r, 0.07 + width(i) * CY)
+
+    def gat(q, o, win, off, scale=1.0):
+        if q == "V":
+            f = lambda: g.vector.tensor_copy(o[0], win[0].indirect(off[0]))
+        else:
+            f = lambda: g.scalar.activation(o[0], win[0].indirect(off[0]), AF.Copy, 0.0, scale)
+        add(q, [f], [o[1]], [win[1], off[1]], 0.07 + 16 * width(off) * GA * CY)
+
+    def gatop(o, win, off, b, op):
+        add("V", [lambda: g.vector.tensor_tensor(o[0], win[0].indirect(off[0]), b[0], op)], [o[1]], [win[1], off[1], b[1]], 0.07 + 16 * width(off) * GA * CY)
+
+    def pe(out, terms, first=True, last=True):
+        calls, regs, n, c = [], [], len(terms), 0.05
+        for k, (po, l, r) in enumerate(terms):
+            calls.append(lambda po=po, l=l, r=r, k=k: g.tensor.matmul(po[0], l[0], r[0], first and k == 0, last and k == n - 1))
+            regs += [l[1], r[1]]
+            c += max(64, width(po)) * PEC
+        add("P", calls, [out[1]], sorted(set(regs)), c)
+
+    def spread(out_name, lo, src):
+        calls, regs = [], [src[1]]
+        w = 16 * width(src)
+        for rho in range(16):
+            po = A(out_name, lo + rho, lo + w, 16)
+            l = A("R", rho * 128, rho * 128 + 128)
+            calls.append(lambda po=po, l=l: g.tensor.matmul(po[0], l[0], src[0], True, True))
+            regs.append(l[1])
+        add("P", calls, [(out_name, lo, lo + w, 1)], regs, 0.05 + 16 * 64 * PEC)
+
+    def collect(out, src, lo):
+        pe(out, [(out, A("SF", rho * 128, rho * 128 + 128), A(src, lo + rho, lo + 256, 16)) for rho in range(16)])
+
+    dn = [0]
+
+    def dma(q, o, i, lat, regs_w, regs_r, acc=False):
+        sem = "d%d" % dn[0]
+        dn[0] += 1
+        if acc:
+            f = lambda: g.dma_start(o, i, accum_op=OP.add, max_dma_last_dim=4096)
+        else:
+            f = lambda: queues[q].dma_start(o, i)
+        add(q, [f], regs_w, regs_r, 1.0 if q == "G" else 0.1, lat, "d", sem, 16)
+
+    def load(q, name, src, lat, hi=None):
+        a = A(name, 0, hi)
+        dma(q, a[0], T[src][:], lat, [a[1]], [])
+
+    load("Y", "hki", "hk", 2.2)
+    load("S", "wti", "wt", 2.2)
+    load("Y", "zin0", "zc", 2.4)
+    load("S", "thi", "th", 2.4)
+    load("Y", "gist", "gi", 4.0, E)
+    load("Y", "ixi", "ix", 6.0)
+    load("Y", "lki", "lk", 7.0)
+    load("Y", "xcb", "xc", 8.0)
+
+    def aff(o, i, pat, op, base, cm, fill=0.0):
+        add("G", [lambda: g.affine_select(o[0], i[0], pat, op, fill, base, cm)], [o[1]], [i[1]], 0.2 + 2 * width(i) * CY)
+
+    def iot(o, pat, base, cm):
+        add("G", [lambda: g.iota(o[0], pat, base, cm, allow_small_or_imprecise_dtypes=True)], [o[1]], [], 0.16 + 2 * width(o) * CY)
+
+    def rep(name, n, w):
+        k = w
+        while k < n:
+            cp(A(name, k, 2 * k), A(name, 0, k))
+            k *= 2
+
+    head[0] = 50.0
+    ms(A("one"), 1.0)
+    ms(A("SW"), 0.0)
+    ms(A("R"), 1.0)
+    head[0] = 0.0
+    ms(A("S"), 0.0)
+    head[0] = 50.0
+    aff(A("blk"), A("one"), [[-16, 8], [0, 16]], OP.is_ge, 0, 1)
+    aff(A("blk"), A("blk"), [[16, 8], [0, 16]], OP.is_ge, 15, -1)
+    aff(A("idf"), A("one"), [[-1, 128]], OP.is_equal, 0, 1)
+    tt(A("pm64"), A("idf", 0, 64), A("idf", 64, 128), OP.add)
+    tt(A("pm32"), A("pm64", 0, 32), A("pm64", 32, 64), OP.add)
+    tt(A("pm"), A("pm32", 0, 16), A("pm32", 16, 32), OP.add)
+    cp(A("wtf"), A("wti"))
+    ts(A("wblk"), A("blk"), A("wtf"), OP.mult)
+    for k in range(16):
+        cp(A("SW", k * 129, k * 128 + 128, 16), A("wblk", 0, 128, 16))
+    head[0] = 0.0
+    for k in range(16):
+        act(A("S", k * 129, k * 128 + 128, 16), A("blk", 0, 128, 16), AF.Copy)
+    cp(A("hkf"), A("hki"))
+    cp(A("thf"), A("thi"))
+    for k in range(0, 16, 4):
+        aff(A("R", k * 128, k * 128 + 512), A("R", k * 128, k * 128 + 512), [[-1, 4], [-16, 8], [0, 16]], OP.is_equal, -k, 1)
+    iot(A("im"), [[1, 16]], 0, 0)
+    ts(A("pd", 0, 16), A("pm"), A("hkf", 0, 1), OP.mult)
+    ts(A("pd", 16, 32), A("pm"), A("thf", 0, 1), OP.mult)
+    pe(A("ps5", 64, 96), [(A("ps5", 64, 96), A("blk"), A("pd"))])
+    cp(A("prow", 0, 16), A("ps5", 64, 80))
+    rep("prow", 128, 16)
+    cp(A("imr", 0, 16), A("im"))
+    rep("imr", 128, 16)
+    ms(A("c8k"), -8192.0)
+    ts(A("r0k"), A("R", 0, 128), 2048.0, OP.mult)
+    ms(A("rmin"), -4.0e7)
+    ms(A("rmin", 0, 128, 16), 4.0e7)
+    ms(A("zer"), 0.0)
+    for name, c, off in (("idb", 1.0, 0), ("nib", -1.0, 0), ("id16", 1.0, 0), ("ni16", -1.0, 0), ("hi16", 0.5, 0), ("nh16", -0.5, 0), ("k1b", 1024.0, 0), ("sh16", 1.0, -1)):
+        aff(A(name), A("zer"), [[-1, 128]], OP.not_equal, off, 1, c)
+    aff(A("D"), A("R"), [[1, 16], [0, 8], [-1, 16]], OP.is_equal, 0, 0)
+    ms(A("nx0", 2048, 2064), 0.0)
+    ms(A("nx1", 2048, 2064), 0.0)
+    ms(A("rz"), -100.0)
+    ms(A("rz", 0, 2048, 16), 100.0)
+    ms(A("half"), 0.5)
+    ms(A("zero"), 0.0)
+    scan(A("pw"), A("half"), A("zero"), 2.0, OP.mult, OP.add)
+    tt(A("tw"), A("pw"), A("pm"), OP.mult)
+    total_of(A("wcol"), A("tw"))
+    tt(A("tr"), A("im"), A("pm"), OP.mult)
+    total_of(A("rcol"), A("tr"))
+    act(A("wd"), A("blk"), AF.Copy, A("wcol"))
+    act(A("bo4"), A("blk"), AF.Copy, 4.0)
+    ts(A("thr", 0, 16), A("pw"), 2.0, OP.mult)
+    rep("thr", 256, 16)
+    iot(A("lan0"), [[16, 16]], E, 0)
+    ts(A("lane", 0, 16), A("lan0"), A("rcol"), OP.add)
+    ts(A("lane", 16, 32), A("lane", 0, 16), float(E - W), OP.subtract)
+    ts(A("kcol"), A("rcol"), -1.0, OP.mult, 15.0, OP.add)
+    cp(A("SF"), A("S"))
+    if "V" in FPLAN:
+        for k in range(0, 2048, 1024):
+            act(A("NS", k, k + 1024), A("S", k, k + 1024), AF.Copy, -1.0)
+    ts(A("ksr", 0, 16), A("im"), -1.0, OP.mult, 15.0, OP.add)
+    ts(A("akey", 0, 16), A("ps5", 80, 96), 16.0, OP.mult)
+    tt(A("akey", 0, 16), A("akey", 0, 16), A("ksr", 0, 16), OP.add)
+    ms(A("ksr", 15, 16), -32768.0)
+    ms(A("akey", 15, 16), -1.0e6)
+    rep("ksr", 128, 16)
+    rep("akey", 128, 16)
+    ms(A("rmax"), 4.0e7)
+    ms(A("rmax", 0, 128, 16), -4.0e7)
+    ms(A("rcnt"), 1.0)
+    ms(A("rcnt", 0, 128, 16), 0.0)
+    ms(A("oneb"), 1.0)
+    cp(A("bo16"), A("blk"))
+    ts(A("thf", 1, 2), A("thf", 1, 2), -1.0, OP.mult, -0.5, OP.add)
+    ts(A("nb16"), A("idf"), A("thf", 1, 2), OP.mult)
+    ms(A("one16"), 1.0)
+
+    def quad(name, c0, c1):
+        return (T[name][:, c0:c1, :, :], (name, c0 * 256, c1 * 256, 1))
+
+    def line(name, rho):
+        return (T[name][:, :, rho, :], (name, 0, 2048, 1))
+
+    bank = [0]
+
+    def plan(s):
+        return [(q, 64 * k, 64) for k, q in enumerate(s)]
+
+    def absdiff(parts, win, off, raw, other, sub, dest, scale):
+        for (q, l0, n) in parts:
+            h, a, b = l0 // 128, (l0 % 128) * 16, (l0 % 128 + n) * 16
+            head[0] = HEAD * (1 - h)
+            o = A("%s%d" % (raw, h), a, b)
+            if q == "V":
+                gatop(o, win, A(off, l0, l0 + n), other(h, a, b), OP.subtract if sub else OP.add)
+                for x in range(a, b, 1024):
+                    act(quad("%s%d" % (dest, h), x // 256, min(x + 1024, b) // 256), A("%s%d" % (raw, h), x, min(x + 1024, b)), AF.Abs, scale)
+            else:
+                gat("S", o, win, A(off, l0, l0 + n))
+                for x in range(a, b, 512):
+                    y = min(x + 512, b)
+                    ps = A("ps%d" % bank[0], 0, y - x)
+                    bank[0] ^= 1
+                    pe(ps, [(ps, A("idb"), A("%s%d" % (raw, h), x, y)), (ps, A("nib" if sub else "idb"), other(h, x, y))])
+                    act(quad("%s%d" % (dest, h), x // 256, y // 256), ps, AF.Abs, scale)
+
+    def firsts(bc, own, eqn, lo_lo, small, extra=None):
+        bank7 = (None, ("ps7", 0, 512, 1))
+        O = lambda x, y: A("ps7", 256 + x, 256 + y)
+        E3 = lambda c, x, y: (T[eqn][:, c, x:y], (eqn, 256 * c + x, 256 * c + y, 1))
+        if extra:
+            pe(bank7, [(O(0, 256),) + extra], True, False)
+        else:
+            rest = []
+        for c0, c1 in ((0, 3), (3, 7), (7, 11), (11, 16)):
+            calls, w, r, cost = [], [], [], 0.0
+            for c in range(c0, c1):
+                o = E3(c, 0, 256 - 16 * c)
+                i = A(bc, 16 * c, 256)
+                s = A(own, c, c + 1)
+                calls.append(lambda o=o, i=i, s=s: g.vector.tensor_scalar(o[0], i[0], s[0], None, OP.is_equal))
+                w.append(o[1])
+                r += [i[1], s[1]]
+                cost += vcost(256 - 16 * c, 0.5) - 0.03
+            add("V", calls, w, sorted(set(r)), cost)
+            terms = [(O(16 * c + 16, 256), A("bo4"), E3(c, 16, 256 - 16 * c)) for c in range(c0, min(c1, 15))]
+            if extra:
+                pe(bank7, terms, False, False)
+            else:
+                rest += terms
+        own_block = (O(0, 256), A("wd"), (T[eqn][:, :, 0:16], (eqn, 0, 4096, 1)))
+        if extra:
+            pe(bank7, [own_block], False, True)
+        else:
+            pe(bank7, [own_block] + rest)
+        tt(A("lo", lo_lo, lo_lo + 256), O(0, 256), A("thr"), OP.is_ge)
+        collect(A("ps5", small, small + 16), "lo", lo_lo)
+
+    def sel(k, own, t, dlt):
+        tt(A("dT", 16 * k, 16 * k + 16), t, dlt, OP.mult)
+        tt(A("oT", 16 * k, 16 * k + 16), A("dT", 16 * k, 16 * k + 16), own, OP.add)
+        cp(A("of", 16 * k, 16 * k + 16), A("oT", 16 * k, 16 * k + 16))
+
+    def scat(win, off, src, src2=None):
+        if src2 is None:
+            f = lambda: g.vector.tensor_copy(win[0].indirect(off[0]), src[0])
+        else:
+            f = lambda: g.vector.tensor_tensor(win[0].indirect(off[0]), src[0], src2[0], OP.add)
+        add("V", [f], [win[1]], [off[1], src[1]] + ([src2[1]] if src2 else []), 0.06 + 256 * SC * CY)
+
+    def cues(t):
+        head[0] = HC
+        z, cb, v16 = "zin%d" % t, "cmb%d" % (t & 1), "v16%d" % (t & 1)
+        u = A("ps6", 0, 16)
+        pe(u, [(u, A("SW", r * 128, r * 128 + 128), A(z, r, 256, 16)) for r in range(16)])
+        cp(A("ui", 0, 16), u)
+        ts(A("ui", 16, 32), A("ui", 0, 16), 4095, OP.bitwise_and)
+        tt(A("sq"), A("ui", 16, 32), A("ui", 16, 32), OP.mult)
+        ts(A(cb, 0, 16), A("ui", 0, 16), 2047, OP.bitwise_and)
+        ts(A(cb, 16, 32), A("sq"), 5, OP.logical_shift_right, 2047, OP.bitwise_and)
+        ts(A(cb, 32, 48), A("sq"), 4, OP.logical_shift_right, 1023, OP.bitwise_and)
+        cp(A("cf"), A(cb))
+        spread("ps6", 0, A("cf", 0, 32))
+        act(A("xe"), A("ps6", 0, 256), AF.Copy, A("hkf", 0, 1))
+        act(A("xq"), A("ps6", 0, 256), AF.Copy, A("hkf", 1, 2))
+        tt(A("ei" if t == 0 else "e0"), A("ps6", 256, 512), A("xe"), OP.add)
+        spread("ps6", 0, A("cf", 32, 48))
+        tt(A("vi"), A("ps6", 0, 256), A("xq"), OP.add)
+        ts(A("vj"), A("vi"), 1023, OP.bitwise_and)
+        cp(A(v16), A("vj"))
+        zr = "zr%d" % (t & 1)
+        head[0] = 0.0
+        for k in range(0, 16, 4):
+            if ZPLAN[t][k // 4] == "S":
+                add("S", [lambda m=m: g.scalar.activation(T[zr][:, m::16], T[z][:], AF.Copy, 0.0, 1.0) for m in range(k, k + 4)],
+                    [(zr, m, 4096, 16) for m in range(k, k + 4)], [(z, 0, 256, 1)], 4 * (0.07 + 256 * CY))
+            else:
+                add("V", [lambda m=m: g.vector.tensor_copy(T[zr][:, m::16], T[z][:]) for m in range(k, k + 4)],
+                    [(zr, m, 4096, 16) for m in range(k, k + 4)], [(z, 0, 256, 1)], 4 * vcost(256, 0.5))
+
+    cues(0)
+    H = ((0, 0, 128), (1, 128, 256))
+    for t in range(RO):
+        z, zr, cb = "zin%d" % t, "zr%d" % (t & 1), "cmb%d" % (t & 1)
+        for (h, a, b) in H:
+            if t:
+                ts(A("ei", a, b), A("e0", a, b), A("acol"), OP.add)
+            ts(A("ej", a, b), A("ei", a, b), 2047, OP.bitwise_and)
+            cp(A("e16", a, b), A("ej", a, b))
+        if t:
+            ts(A("bs"), A(cb, 16, 32), A("acol"), OP.add)
+        base, boff = ("bs", 0) if t else (cb, 16)
+        absdiff(plan(GPLAN[t]), A("gist", 0, E), "e16", "gd", lambda h, x, y: A(zr, h * 2048 + x, h * 2048 + y), True, "aa", 32768.0)
+        for (h, a, b) in H:
+            head[0] = HEAD * (1 - h)
+            c0, c1 = 8 * h, 8 * h + 8
+            k = A("ps%d" % (2 + h), 0, 128)
+            pe(k, [(k, A("R", 0, 128), A("prow")), (k, A("r0k"), A("imr")), (k, A("r0k"), A("c8k"))]
+               + [(k, A("S", r * 128, r * 128 + 128), line("aa%d" % h, r)) for r in range(16)])
+            scan(A("km%d" % h), A("rmin"), k, 4.0e7, OP.max, OP.min)
+            i0, i1, i2, i3 = [A("ki", 32 * h + 8 * x, 32 * h + 8 * x + 8) for x in range(4)]
+            cp(i0, A("km%d" % h, 15, 128, 16))
+            ts(i1, i0, 2047, OP.bitwise_and)
+            tt(i2, i1, A(cb, c0, c1), OP.mult)
+            tt(i3, i2, A(base, boff + c0, boff + c1), OP.add)
+            ts(A("el", c0, c1), i3, 2047, OP.bitwise_and)
+            cp(A("elu", c0, c1), A("el", c0, c1))
+            gat("V", A("ju", a, b), A("nm", 0, E) if t else A("ixi"), A("elu", c0, c1))
+            for q in (0, 64):
+                gat("V", A("lg%d" % h, 16 * q, 16 * q + 1024), A("lkt", 0, W) if t else A("lki"), A("ju", a + q, a + q + 64))
+                gat("S", A("nx%d" % h, 16 * q, 16 * q + 1024), A("xcb"), A("ju", a + q, a + q + 64), -1.0)
+                n = A("ps%d" % (2 + h), 128 + q, 192 + q)
+                pe(n, [(n, A("D", r * 128, r * 128 + 128), A("lg%d" % h, 16 * q + r, 16 * q + 1024, 16)) for r in range(16)])
+                cp(A("nu", a + q, a + q + 64), n)
+            cp(A("jh", a, b), A("ju", a, b))
+            cp(A("nh", a, b), A("nu", a, b))
+            head[0] = HZ
+            scan(A("zs%d" % h), A("rz"), A("nx%d" % h, 0, 2048), 100.0, OP.max, OP.min)
+            zp = A("ps6", a, b)
+            pe(zp, [(zp, A("idb"), A(z, a, b)), (zp, A("nib"), A("zs%d" % h, 15, 2048, 16))])
+            act(A("ze", a, b), zp, AF.Copy, 0.5, 127.75)
+            act(A("zo%d" % t, a, b), A("ze", a, b), AF.Copy, 1.0, -128.0)
+        dst = T.cores[(rank + 1) % len(T.cores)] if t < RO - 1 else T.cores[(rank - t) % len(T.cores)]
+        land = "zin%d" % (t + 1) if t < RO - 1 else "zfin"
+        eng = topo.engines(core, dst)[:NENG]
+        rid, pid, _se = topo.addr(dst)
+        mask = sum(1 << e for e in eng)
+        add("G", [lambda land=land, rid=rid, pid=pid, mask=mask, t=t: g.remote_dma(
+            T[land][:], T["zo%d" % t][:], T.sem["arr%d" % (t + 1)], T.sem.snd, pid, rid, mask)],
+            [(land, 0, 256, 1)], [("zo%d" % t, 0, 256, 1)], 1.0, 3.0, "r", "arr%d" % (t + 1), len(eng))
+        head[0] = 0.0
+        for (h, a, b) in H:
+            x = A(zr, h * 2048, h * 2048 + 2048)
+            dma("G", x[0], T["nx%d" % h][:, 0:2048], 5.0, [x[1]], [x[1], ("nx%d" % h, 0, 2048, 1)], acc=True)
+        cp(A("elf"), A("el"))
+        cp(A("elh"), A("el"))
+        tt(A("dE", 0, 16), A("lane", 0, 16), A("elf"), OP.subtract)
+        spread("ps7", 0, A("elh"))
+        cp(A("eB"), A("ps7", 0, 256))
+        firsts("eB", "elf", "eq", 0, 32)
+        ts(A("loL"), A("ps5", 32, 48), 0.0625, OP.mult)
+        sel(0, A("elf"), A("loL", 0, 16), A("dE", 0, 16))
+        for (h, a, b) in H:
+            c0, c1 = 8 * h, 8 * h + 8
+            absdiff([p for p in plan(YPLAN[t]) if p[1] // 128 == h], A("xcb"), "nu", "yb", lambda h, x, y: A("nx%d" % h, x + 1, y + 1), False, "ya", 16.0)
+            k = A("ps%d" % (2 + h), 256, 384)
+            pe(k, [(k, A("R", 0, 128), A("ksr"))] + [(k, A("S", r * 128, r * 128 + 128), line("ya%d" % h, r)) for r in range(16)])
+            tt(A("cm%d" % h), k, A("akey"), OP.is_le)
+            scan(A("cn%d" % h), A("rcnt"), A("cm%d" % h), 0.0, OP.mult, OP.add)
+            ts(A("rec", c0, c1), A("cn%d" % h, 15, 128, 16), float(NEED), OP.is_ge)
+            cp(A("recb", c0, c1), A("rec", c0, c1))
+            scan(A("kx%d" % h), A("rmax"), k, -4.0e7, OP.min, OP.max)
+            cp(A("kj", c0, c1), A("kx%d" % h, 15, 128, 16))
+            ts(A("kj", 16 + c0, 16 + c1), A("kj", c0, c1), 15, OP.bitwise_and)
+        head[0] = 0.0
+        if t < RO - 1:
+            cues(t + 1)
+            cnt = A("ps3", 384, 400)
+            pe(cnt, [(cnt, A("oneb"), A("recb"))])
+            total_of(A("acol"), cnt)
+            ts(A("nrec"), A("rec"), -1.0, OP.mult, 1.0, OP.add)
+            tt(A("gT"), A("loL", 0, 16), A("nrec"), OP.max)
+            sel(1, A("elf"), A("gT"), A("dE", 0, 16))
+            scat(A("gist"), A("of", 16, 32), A(z))
+        F = A("ps4", 0, 256)
+        jp = A("ps4", 256, 512)
+        pe(jp, [(jp, A("id16"), A("jh"))])
+        pe((None, ("ps4", 0, 512, 1)), [(F, A("nb16"), A("one16"))], True, False)
+        for (h, a, b) in H:
+            fh = A("ps4", a, b)
+            terms = [(fh, A("S", r * 128, r * 128 + 128), A("fa%d" % h, r, 2048, 16)) for r in range(16)]
+            if FPLAN[h] == "S":
+                for x in (0, 1024):
+                    act(A("fa%d" % h, x, x + 1024), A(zr, h * 2048 + x, h * 2048 + x + 1024), AF.Abs)
+            else:
+                for x in (0, 1024):
+                    ts(A("fa%d" % h, x, x + 1024), A(zr, h * 2048 + x, h * 2048 + x + 1024), 0.0, OP.max, 2.0, OP.mult)
+                terms += [(fh, A("NS", r * 128, r * 128 + 128), A(zr, h * 2048 + r, h * 2048 + 2048, 16)) for r in range(16)]
+            pe(fh, terms, False, False)
+        ts(A("rec"), A("rec"), 16.0, OP.mult)
+        tt(A("jr"), A("kj", 16, 32), A("rec"), OP.add)
+        spread("ps5", 256, A("jr"))
+        act(A("rB"), A("ps5", 256, 512), AF.Relu, 1.0, -15.0)
+        ts(A("oh"), A("ps5", 256, 512), A("kcol"), OP.is_equal)
+        tt(A("pj"), A("ps4", 256, 512), A("oh"), OP.mult)
+        pe(F, [(F, A("k1b"), A("rB"))], False, True)
+        dp, ib = A("ps6", 0, 256), A("ps6", 256, 512)
+        pe(ib, [(ib, A("bo16"), A("pj")), (ib, A("k1b"), A("rB"))])
+        cp(A("IB"), ib)
+        pe(dp, [(dp, A("sh16"), A("jh")), (dp, A("ni16"), A("nh"))])
+        tt(A("dl"), dp, A("oh"), OP.mult)
+        v = A("v16%d" % (t & 1))
+        hp, hm = A("ps6", 0, 256), A("ps6", 256, 512)
+        pe(hp, [(hp, A("hi16"), v), (hp, A("hi16"), A("jh"))])
+        act(A("ja"), hp, AF.Copy)
+        pe(hm, [(hm, A("hi16"), v), (hm, A("nh16"), A("jh"))])
+        act(A("mk"), F, AF.Sign)
+        tt(A("pn"), hm, A("mk"), OP.mult)
+        if t == 0:
+            for x in range(0, E, 512):
+                cp(A("nm", x, x + 512), A("ixi", x, x + 512))
+            for x in range(0, W, 512):
+                cp(A("lkt", x, x + 512), A("lki", x, x + 512))
+        scat(A("nm"), A("of", 0, 16), A("pn"), A("ja"))
+        collect(A("ps5", 48, 64), "pj", 0)
+        cp(A("ILu"), A("ps5", 48, 64))
+        ts(A("dT", 48, 64), A("rec"), 128.0, OP.mult)
+        tt(A("IL"), A("ps5", 48, 64), A("dT", 48, 64), OP.add)
+        gatop(A("nl"), A("lkt", 0, W), A("ILu"), A("dl"), OP.add)
+        tt(A("dE", 16, 32), A("lane", 16, 32), A("IL"), OP.subtract)
+        ts(A("dE", 16, 32), A("dE", 16, 32), 0.0625, OP.mult)
+        firsts("IB", "IL", "eq2", 256, 96, (A("k1b"), A("rB")))
+        sel(2, A("IL"), A("ps5", 96, 112), A("dE", 16, 32))
+        scat(A("lkt"), A("of", 32, 48), A("nl"))
+    dma("Y", T.yz[:], T.zfin[:], 2.5, [], [("zfin", 0, 256, 1)])
+    dma("Y", T.yi[:], T.nm[:, 0:E], 5.0, [], [("nm", 0, E, 1)])
+    dma("Y", T.yl[:], T.lkt[:, 0:W], 3.5, [], [("lkt", 0, W, 1)])
+
+    n = len(ops)
+    users = [[] for _ in range(n)]
+    for o in ops:
+        for d in o["deps"]:
+            users[d].append(o["i"])
+    WAKE = 0.08
+    way = [0.0] * n
+    for i in range(n - 1, -1, -1):
+        o = ops[i]
+        way[i] = o["cost"] + o["lat"] + max([way[j] + WAKE for j in users[i]] + [0.0])
+    queue, cost = [o["q"] for o in ops], [o["cost"] for o in ops]
+    tail = [o["cost"] + o["lat"] for o in ops]
+    then = [[(j, tail[i] + WAKE if ops[j]["deps"][i] else 1e-6) for j in users[i]] for i in range(n)]
+    npre = [len(o["deps"]) for o in ops]
+
+    def place(key):
+        left, avail, start, order = list(npre), [0.0] * n, [0.0] * n, []
+        free, ready = {q: 0.0 for q in queues}, {q: [] for q in queues}
+        for i in range(n):
+            if left[i] == 0:
+                ready[queue[i]].append(i)
+        while len(order) < n:
+            m, q = 1e18, None
+            for x in ready:
+                if ready[x]:
+                    y = max(free[x], min(avail[i] for i in ready[x]))
+                    if y < m:
+                        m, q = y, x
+            i = max((j for j in ready[q] if avail[j] <= m + LOOK), key=lambda j: key[j])
+            s = start[i] = max(avail[i], free[q])
+            free[q] = s + cost[i]
+            ready[q].remove(i)
+            order.append(i)
+            for j, w in then[i]:
+                left[j] -= 1
+                if s + w > avail[j]:
+                    avail[j] = s + w
+                if left[j] == 0:
+                    ready[queue[j]].append(j)
+        return start, order, max(start[i] + tail[i] for i in range(n))
+
+    if n not in ORDER:
+        key = [way[i] + ops[i]["head"] for i in range(n)]
+        best = place(key)
+        rng = np.random.RandomState(5)
+        for k in range(TRIES):
+            nk = [float(x) for x in np.array(key) + (rng.rand(n) < (0.02, 0.1, 0.4)[k % 3]) * rng.randn(n) * (0.5, 2.0, 6.0)[(k // 3) % 3]]
+            new = place(nk)
+            if new[2] <= best[2]:
+                key, best = nk, new
+        ORDER[n] = best
+    start, order, _span = ORDER[n]
+    fin = [start[i] + tail[i] for i in range(n)]
+
+    know = {q: {} for q in queues}
+    clock = [None] * n
+    count = {q: 0 for q in queues}
+    total = {}
+    for i in order:
+        o = ops[i]
+        q = o["q"]
+        k = know[q]
+        for d in sorted(o["deps"]):
+            if not o["deps"][d]:
+                continue
+            sem, val, ck = clock[d]
+            if k.get(sem, 0) < val:
+                queues[q].wait_ge(T.sem[sem], val)
+                k[sem] = val
+                for s2, v2 in ck.items():
+                    if k.get(s2, 0) < v2:
+                        k[s2] = v2
+        ck = dict(k)
+        inst = None
+        for f in o["calls"]:
+            inst = f()
+        if o["kind"] == "c":
+            count[q] += 1
+            inst.then_inc(T.sem["e" + q], 1)
+            clock[i] = ("e" + q, count[q], ck)
+            total["e" + q] = count[q]
+        elif o["kind"] == "d":
+            inst.then_inc(T.sem[o["sem"]], 16)
+            clock[i] = (o["sem"], 16, ck)
+            total[o["sem"]] = 16
+        else:
+            clock[i] = (o["sem"], o["val"], {})
+            total[o["sem"]] = o["val"]
+            total["snd"] = total.get("snd", 0) + o["val"]
+    for sem in sorted(total):
+        if know["G"].get(sem, 0) < total[sem]:
+            g.wait_ge(T.sem[sem], total[sem])

@@ -3,12 +3,12 @@ from concourse.mybir import AluOpType as OP, ActivationFunctionType as AF, AxisL
 
 W, E, B, RO, NEED = 1024, 2048, 256, 3, 11
 NENG = 4
-GPLAN = ("VSVS", "SSSV", "SSSV")
-YPLAN = ("SSSV", "SSSV", "SSSV")
-ZPLAN = ("VSVS", "VSVS", "VSVS")
+GPLAN = ("SVSV", "SVSV", "VSVS")
+YPLAN = ("SVSV", "SSSV", "SVSV")
+ZPLAN = ("VVVV", "VGVG", "VVVG")
 FPLAN = "SS"
-TRIES, ORDER = 500, {}
-HEAD, HZ, HC, LOOK = 5.0, 8.0, 8.0, 0.05
+TRIES, ORDER = 2000, {}
+HEAD, HZ, HC, LOOK = 0.0, 2.0, 6.0, 0.04
 F32, BF, F16, I32, U16 = "float32", "bfloat16", "float16", "int32", "uint16"
 
 SCRATCH = {
@@ -29,15 +29,15 @@ for _k in (0, 1):
 _SMALL = {
     F32: (("wtf", 1), ("hkf", 2), ("thf", 2), ("one", 128), ("idf", 128), ("blk", 128), ("wblk", 128), ("zer", 128), ("pm64", 64), ("pm32", 32), ("pm", 16), ("im", 16),
           ("half", 16), ("zero", 16), ("pw", 16), ("tw", 16), ("tr", 16), ("wcol", 1), ("rcol", 1), ("kcol", 1), ("thr", 256), ("lane", 32), ("lan0", 16),
-          ("pd", 32), ("akey", 128), ("rmin", 128), ("rmax", 128), ("xe", 256), ("xq", 256), ("e0", 256), ("km0", 128), ("km1", 128), ("elf", 16),
-          ("ja", 256), ("kx0", 128), ("kx1", 128), ("rec", 16), ("nrec", 16), ("acol", 1), ("loL", 16), ("dE", 32), ("dT", 64), ("oT", 64), ("gT", 16),
+          ("pd", 32), ("akey", 128), ("rmin", 128), ("rmax", 128), ("xe", 256), ("xq", 256), ("e0", 256), ("elf", 16),
+          ("ja", 256), ("rec", 16), ("nrec", 16), ("acol", 1), ("loL", 16), ("dE", 32), ("dT", 64), ("oT", 64), ("gT", 16),
           ("IL", 16), ("dl", 256), ("nl", 256), ("pn", 256)),
-    F16: (("id16", 128), ("ni16", 128), ("hi16", 128), ("nh16", 128), ("sh16", 128), ("bo16", 128), ("nb16", 128), ("one16", 256), ("r0k", 128), ("prow", 128), ("imr", 128), ("c8k", 128),
+    F16: (("id16", 128), ("ni16", 128), ("hi16", 128), ("nh16", 128), ("sh16", 128), ("bo16", 128), ("nb16", 128), ("one16", 512), ("r0k", 128), ("prow", 128), ("imr", 128), ("c8k", 128),
           ("ksr", 128), ("cf", 48), ("v160", 256), ("v161", 256), ("elh", 16), ("jh", 256), ("nh", 256), ("jr", 16), ("eB", 256), ("IB", 256), ("lo", 512),
           ("oh", 256), ("pj", 256)),
-    BF: (("idb", 128), ("nib", 128), ("k1b", 128), ("oneb", 128), ("wd", 128), ("bo4", 128), ("rcnt", 128), ("ze", 256), ("cm0", 128), ("cm1", 128), ("cn0", 128), ("cn1", 128),
+    BF: (("idb", 128), ("nib", 128), ("k1b", 128), ("oneb", 128), ("wd", 128), ("bo4", 128), ("rcnt", 128), ("ze", 256), ("cm0", 128), ("cm1", 128), ("cn", 256),
          ("recb", 16), ("rB", 256), ("mk", 256)),
-    I32: (("ui", 32), ("sq", 16), ("cmb0", 48), ("cmb1", 48), ("bs", 16), ("ei", 256), ("ej", 256), ("vi", 256), ("vj", 256), ("ki", 64), ("el", 16), ("kj", 32)),
+    I32: (("kx", 256), ("km0", 128), ("km1", 128), ("ui", 32), ("sq", 16), ("cmb0", 48), ("cmb1", 48), ("bs", 16), ("ei", 256), ("ej", 256), ("vi", 256), ("vj", 256), ("ki", 64), ("el", 16), ("kj", 32)),
     U16: (("e16", 256), ("elu", 16), ("ju", 256), ("nu", 256), ("of", 64), ("ILu", 16)),
 }
 PLACE = {}
@@ -52,8 +52,8 @@ for _k in range(8):
 NDMA = 20
 SEMAPHORES = ["eV", "eS", "eP", "eG", "snd", "arr1", "arr2", "arr3"] + ["d%d" % k for k in range(NDMA)]
 
-CY = 0.00083 * 1.25
-GA, SC, PEC = 1.56, 3.8, 0.0006
+CY = 0.00083 * 1.15
+GA, SC, PEC, VO, WAKE = 1.4, 3.0, 0.0005, 0.03, 0.06
 
 
 def rank_program(g, core, T, topo):
@@ -96,7 +96,7 @@ def rank_program(g, core, T, topo):
         ops.append(o)
 
     def vcost(n, f=1.0):
-        return 0.06 + max(64.0, n * f) * CY
+        return VO + max(64.0, n * f) * CY
 
     def width(x):
         return (x[1][2] - x[1][1] + x[1][3] - 1) // x[1][3]
@@ -193,22 +193,27 @@ def rank_program(g, core, T, topo):
     def aff(o, i, pat, op, base, cm, fill=0.0):
         add("G", [lambda: g.affine_select(o[0], i[0], pat, op, fill, base, cm)], [o[1]], [i[1]], 0.2 + 2 * width(i) * CY)
 
+    def gcp(o, i):
+        add("G", [lambda: g.affine_select(o[0], i[0], [[1, width(o)]], OP.is_ge, 0.0, 1, 0)], [o[1]], [i[1]], 0.2 + 2 * width(o) * CY)
+
     def iot(o, pat, base, cm):
         add("G", [lambda: g.iota(o[0], pat, base, cm, allow_small_or_imprecise_dtypes=True)], [o[1]], [], 0.16 + 2 * width(o) * CY)
 
-    def rep(name, n, w):
+    def rep(name, n, w, cp=cp):
         k = w
         while k < n:
             cp(A(name, k, 2 * k), A(name, 0, k))
             k *= 2
 
-    head[0] = 50.0
+    head[0] = 80.0
     ms(A("one"), 1.0)
+    head[0] = 70.0
+    ms(A("one16"), 1.0)
     ms(A("SW"), 0.0)
-    ms(A("R"), 1.0)
     head[0] = 0.0
-    ms(A("S"), 0.0)
-    head[0] = 50.0
+    for k in range(0, 2048, 512):
+        ms(A("S", k, k + 512), 0.0)
+    head[0] = 60.0
     aff(A("blk"), A("one"), [[-16, 8], [0, 16]], OP.is_ge, 0, 1)
     aff(A("blk"), A("blk"), [[16, 8], [0, 16]], OP.is_ge, 15, -1)
     aff(A("idf"), A("one"), [[-1, 128]], OP.is_equal, 0, 1)
@@ -217,15 +222,18 @@ def rank_program(g, core, T, topo):
     tt(A("pm"), A("pm32", 0, 16), A("pm32", 16, 32), OP.add)
     cp(A("wtf"), A("wti"))
     ts(A("wblk"), A("blk"), A("wtf"), OP.mult)
-    for k in range(16):
+    for k in range(0, 16, 2):
         cp(A("SW", k * 129, k * 128 + 128, 16), A("wblk", 0, 128, 16))
+        act(A("SW", k * 129 + 129, k * 128 + 256, 16), A("blk", 0, 128, 16), AF.Copy, A("wtf"))
     head[0] = 0.0
     for k in range(16):
         act(A("S", k * 129, k * 128 + 128, 16), A("blk", 0, 128, 16), AF.Copy)
     cp(A("hkf"), A("hki"))
     cp(A("thf"), A("thi"))
+    head[0] = 60.0
     for k in range(0, 16, 4):
-        aff(A("R", k * 128, k * 128 + 512), A("R", k * 128, k * 128 + 512), [[-1, 4], [-16, 8], [0, 16]], OP.is_equal, -k, 1)
+        aff(A("R", k * 128, k * 128 + 512), A("one16"), [[-1, 4], [-16, 8], [0, 16]], OP.is_equal, -k, 1)
+    head[0] = 0.0
     iot(A("im"), [[1, 16]], 0, 0)
     ts(A("pd", 0, 16), A("pm"), A("hkf", 0, 1), OP.mult)
     ts(A("pd", 16, 32), A("pm"), A("thf", 0, 1), OP.mult)
@@ -244,8 +252,9 @@ def rank_program(g, core, T, topo):
     aff(A("D"), A("R"), [[1, 16], [0, 8], [-1, 16]], OP.is_equal, 0, 0)
     ms(A("nx0", 2048, 2064), 0.0)
     ms(A("nx1", 2048, 2064), 0.0)
-    ms(A("rz"), -100.0)
-    ms(A("rz", 0, 2048, 16), 100.0)
+    for k in range(0, 2048, 512):
+        ms(A("rz", k, k + 512), -100.0)
+        ms(A("rz", k, k + 512, 16), 100.0)
     ms(A("half"), 0.5)
     ms(A("zero"), 0.0)
     scan(A("pw"), A("half"), A("zero"), 2.0, OP.mult, OP.add)
@@ -256,12 +265,13 @@ def rank_program(g, core, T, topo):
     act(A("wd"), A("blk"), AF.Copy, A("wcol"))
     act(A("bo4"), A("blk"), AF.Copy, 4.0)
     ts(A("thr", 0, 16), A("pw"), 2.0, OP.mult)
-    rep("thr", 256, 16)
+    rep("thr", 256, 16, gcp)
     iot(A("lan0"), [[16, 16]], E, 0)
     ts(A("lane", 0, 16), A("lan0"), A("rcol"), OP.add)
     ts(A("lane", 16, 32), A("lane", 0, 16), float(E - W), OP.subtract)
     ts(A("kcol"), A("rcol"), -1.0, OP.mult, 15.0, OP.add)
-    cp(A("SF"), A("S"))
+    for k in range(0, 2048, 512):
+        gcp(A("SF", k, k + 512), A("S", k, k + 512))
     if "V" in FPLAN:
         for k in range(0, 2048, 1024):
             act(A("NS", k, k + 1024), A("S", k, k + 1024), AF.Copy, -1.0)
@@ -270,17 +280,16 @@ def rank_program(g, core, T, topo):
     tt(A("akey", 0, 16), A("akey", 0, 16), A("ksr", 0, 16), OP.add)
     ms(A("ksr", 15, 16), -32768.0)
     ms(A("akey", 15, 16), -1.0e6)
-    rep("ksr", 128, 16)
-    rep("akey", 128, 16)
+    rep("ksr", 128, 16, gcp)
+    rep("akey", 128, 16, gcp)
     ms(A("rmax"), 4.0e7)
     ms(A("rmax", 0, 128, 16), -4.0e7)
     ms(A("rcnt"), 1.0)
     ms(A("rcnt", 0, 128, 16), 0.0)
     ms(A("oneb"), 1.0)
-    cp(A("bo16"), A("blk"))
+    gcp(A("bo16"), A("blk"))
     ts(A("thf", 1, 2), A("thf", 1, 2), -1.0, OP.mult, -0.5, OP.add)
     ts(A("nb16"), A("idf"), A("thf", 1, 2), OP.mult)
-    ms(A("one16"), 1.0)
 
     def quad(name, c0, c1):
         return (T[name][:, c0:c1, :, :], (name, c0 * 256, c1 * 256, 1))
@@ -328,7 +337,7 @@ def rank_program(g, core, T, topo):
                 calls.append(lambda o=o, i=i, s=s: g.vector.tensor_scalar(o[0], i[0], s[0], None, OP.is_equal))
                 w.append(o[1])
                 r += [i[1], s[1]]
-                cost += vcost(256 - 16 * c, 0.5) - 0.03
+                cost += vcost(256 - 16 * c, 0.5)
             add("V", calls, w, sorted(set(r)), cost)
             terms = [(O(16 * c + 16, 256), A("bo4"), E3(c, 16, 256 - 16 * c)) for c in range(c0, min(c1, 15))]
             if extra:
@@ -374,13 +383,16 @@ def rank_program(g, core, T, topo):
         spread("ps6", 0, A("cf", 32, 48))
         tt(A("vi"), A("ps6", 0, 256), A("xq"), OP.add)
         ts(A("vj"), A("vi"), 1023, OP.bitwise_and)
-        cp(A(v16), A("vj"))
+        gcp(A(v16), A("vj"))
         zr = "zr%d" % (t & 1)
         head[0] = 0.0
         for k in range(0, 16, 4):
             if ZPLAN[t][k // 4] == "S":
                 add("S", [lambda m=m: g.scalar.activation(T[zr][:, m::16], T[z][:], AF.Copy, 0.0, 1.0) for m in range(k, k + 4)],
                     [(zr, m, 4096, 16) for m in range(k, k + 4)], [(z, 0, 256, 1)], 4 * (0.07 + 256 * CY))
+            elif ZPLAN[t][k // 4] == "G":
+                for m in range(k, k + 4):
+                    gcp(A(zr, m, 4096, 16), A(z))
             else:
                 add("V", [lambda m=m: g.vector.tensor_copy(T[zr][:, m::16], T[z][:]) for m in range(k, k + 4)],
                     [(zr, m, 4096, 16) for m in range(k, k + 4)], [(z, 0, 256, 1)], 4 * vcost(256, 0.5))
@@ -406,8 +418,7 @@ def rank_program(g, core, T, topo):
                + [(k, A("S", r * 128, r * 128 + 128), line("aa%d" % h, r)) for r in range(16)])
             scan(A("km%d" % h), A("rmin"), k, 4.0e7, OP.max, OP.min)
             i0, i1, i2, i3 = [A("ki", 32 * h + 8 * x, 32 * h + 8 * x + 8) for x in range(4)]
-            cp(i0, A("km%d" % h, 15, 128, 16))
-            ts(i1, i0, 2047, OP.bitwise_and)
+            ts(i1, A("km%d" % h, 15, 128, 16), 2047, OP.bitwise_and)
             tt(i2, i1, A(cb, c0, c1), OP.mult)
             tt(i3, i2, A(base, boff + c0, boff + c1), OP.add)
             ts(A("el", c0, c1), i3, 2047, OP.bitwise_and)
@@ -419,8 +430,8 @@ def rank_program(g, core, T, topo):
                 n = A("ps%d" % (2 + h), 128 + q, 192 + q)
                 pe(n, [(n, A("D", r * 128, r * 128 + 128), A("lg%d" % h, 16 * q + r, 16 * q + 1024, 16)) for r in range(16)])
                 cp(A("nu", a + q, a + q + 64), n)
-            cp(A("jh", a, b), A("ju", a, b))
-            cp(A("nh", a, b), A("nu", a, b))
+            gcp(A("jh", a, b), A("ju", a, b))
+            gcp(A("nh", a, b), A("nu", a, b))
             head[0] = HZ
             scan(A("zs%d" % h), A("rz"), A("nx%d" % h, 0, 2048), 100.0, OP.max, OP.min)
             zp = A("ps6", a, b)
@@ -439,8 +450,8 @@ def rank_program(g, core, T, topo):
         for (h, a, b) in H:
             x = A(zr, h * 2048, h * 2048 + 2048)
             dma("G", x[0], T["nx%d" % h][:, 0:2048], 5.0, [x[1]], [x[1], ("nx%d" % h, 0, 2048, 1)], acc=True)
-        cp(A("elf"), A("el"))
-        cp(A("elh"), A("el"))
+        gcp(A("elh"), A("el"))
+        gcp(A("elf"), A("el"))
         tt(A("dE", 0, 16), A("lane", 0, 16), A("elf"), OP.subtract)
         spread("ps7", 0, A("elh"))
         cp(A("eB"), A("ps7", 0, 256))
@@ -453,12 +464,11 @@ def rank_program(g, core, T, topo):
             k = A("ps%d" % (2 + h), 256, 384)
             pe(k, [(k, A("R", 0, 128), A("ksr"))] + [(k, A("S", r * 128, r * 128 + 128), line("ya%d" % h, r)) for r in range(16)])
             tt(A("cm%d" % h), k, A("akey"), OP.is_le)
-            scan(A("cn%d" % h), A("rcnt"), A("cm%d" % h), 0.0, OP.mult, OP.add)
-            ts(A("rec", c0, c1), A("cn%d" % h, 15, 128, 16), float(NEED), OP.is_ge)
-            cp(A("recb", c0, c1), A("rec", c0, c1))
-            scan(A("kx%d" % h), A("rmax"), k, -4.0e7, OP.min, OP.max)
-            cp(A("kj", c0, c1), A("kx%d" % h, 15, 128, 16))
-            ts(A("kj", 16 + c0, 16 + c1), A("kj", c0, c1), 15, OP.bitwise_and)
+            scan(A("cn", a, b), A("rcnt"), A("cm%d" % h), 0.0, OP.mult, OP.add)
+            scan(A("kx", a, b), A("rmax"), k, -4.0e7, OP.min, OP.max)
+        ts(A("rec"), A("cn", 15, 256, 16), float(NEED), OP.is_ge)
+        cp(A("recb"), A("rec"))
+        ts(A("kj", 16, 32), A("kx", 15, 256, 16), 15, OP.bitwise_and)
         head[0] = 0.0
         if t < RO - 1:
             cues(t + 1)
@@ -472,7 +482,7 @@ def rank_program(g, core, T, topo):
         F = A("ps4", 0, 256)
         jp = A("ps4", 256, 512)
         pe(jp, [(jp, A("id16"), A("jh"))])
-        pe((None, ("ps4", 0, 512, 1)), [(F, A("nb16"), A("one16"))], True, False)
+        pe((None, ("ps4", 0, 512, 1)), [(F, A("nb16"), A("one16", 0, 256))], True, False)
         for (h, a, b) in H:
             fh = A("ps4", a, b)
             terms = [(fh, A("S", r * 128, r * 128 + 128), A("fa%d" % h, r, 2048, 16)) for r in range(16)]
@@ -505,9 +515,9 @@ def rank_program(g, core, T, topo):
         tt(A("pn"), hm, A("mk"), OP.mult)
         if t == 0:
             for x in range(0, E, 512):
-                cp(A("nm", x, x + 512), A("ixi", x, x + 512))
+                gcp(A("nm", x, x + 512), A("ixi", x, x + 512))
             for x in range(0, W, 512):
-                cp(A("lkt", x, x + 512), A("lki", x, x + 512))
+                gcp(A("lkt", x, x + 512), A("lki", x, x + 512))
         scat(A("nm"), A("of", 0, 16), A("pn"), A("ja"))
         collect(A("ps5", 48, 64), "pj", 0)
         cp(A("ILu"), A("ps5", 48, 64))
@@ -528,7 +538,6 @@ def rank_program(g, core, T, topo):
     for o in ops:
         for d in o["deps"]:
             users[d].append(o["i"])
-    WAKE = 0.08
     way = [0.0] * n
     for i in range(n - 1, -1, -1):
         o = ops[i]

import numpy as np
from concourse.mybir import AluOpType as OP, ActivationFunctionType as AF, AxisListType as AX

W, E, B, RO, NEED = 1024, 2048, 256, 3, 11
NENG = 4
GPLAN = ("SVSV", "SVSV", "VSVS")
YPLAN = ("SVSV", "SSSV", "SVSV")
ZPLAN = ("VVVV", "VGVG", "VVVG")
FPLAN = "SS"
TRIES, ORDER = 2000, {}
HEAD, HZ, HC, LOOK = 0.0, 2.0, 6.0, 0.04
F32, BF, F16, I32, U16 = "float32", "bfloat16", "float16", "int32", "uint16"

SCRATCH = {
    "gist": ("sbuf", [128, E + B], BF), "nm": ("sbuf", [128, E + B], F32), "lkt": ("sbuf", [128, W + B], F32),
    "xcb": ("sbuf", [128, W], BF), "ixi": ("sbuf", [128, E], I32), "lki": ("sbuf", [128, W], I32),
    "wti": ("sbuf", [128, 1], I32), "hki": ("sbuf", [128, 2], I32), "thi": ("sbuf", [128, 2], I32),
    "zin0": ("sbuf", [128, B], BF), "zin1": ("sbuf", [128, B], BF), "zin2": ("sbuf", [128, B], BF), "zfin": ("sbuf", [128, B], BF),
    "zo0": ("sbuf", [128, B], BF), "zo1": ("sbuf", [128, B], BF), "zo2": ("sbuf", [128, B], BF),
    "S": ("sbuf", [128, 2048], BF), "SF": ("sbuf", [128, 2048], F16), "SW": ("sbuf", [128, 2048], BF), "D": ("sbuf", [128, 2048], F16), "R": ("sbuf", [128, 2048], F16),
    "NS": ("sbuf", [128, 2048], BF), "rz": ("sbuf", [128, 2048], BF), "zr0": ("sbuf", [128, 4096], BF), "zr1": ("sbuf", [128, 4096], BF),
    "eq": ("sbuf", [128, 16, 256], BF), "eq2": ("sbuf", [128, 16, 256], BF),
}
for _k in (0, 1):
    for _n, _d, _w in (("gd", BF, 2048), ("fa", BF, 2048), ("nx", BF, 2064), ("lg", F16, 2048), ("yb", BF, 2048), ("zs", BF, 2048)):
        SCRATCH["%s%d" % (_n, _k)] = ("sbuf", [128, _w], _d)
    SCRATCH["aa%d" % _k] = ("sbuf", [128, 8, 16, 16], BF)
    SCRATCH["ya%d" % _k] = ("sbuf", [128, 8, 16, 16], BF)
_SMALL = {
    F32: (("wtf", 1), ("hkf", 2), ("thf", 2), ("one", 128), ("idf", 128), ("blk", 128), ("wblk", 128), ("zer", 128), ("pm64", 64), ("pm32", 32), ("pm", 16), ("im", 16),
          ("half", 16), ("zero", 16), ("pw", 16), ("tw", 16), ("tr", 16), ("wcol", 1), ("rcol", 1), ("kcol", 1), ("thr", 256), ("lane", 32), ("lan0", 16),
          ("pd", 32), ("akey", 128), ("rmin", 128), ("rmax", 128), ("xe", 256), ("xq", 256), ("e0", 256), ("elf", 16),
          ("ja", 256), ("rec", 16), ("nrec", 16), ("acol", 1), ("loL", 16), ("dE", 32), ("dT", 64), ("oT", 64), ("gT", 16),
          ("IL", 16), ("dl", 256), ("nl", 256), ("pn", 256)),
    F16: (("id16", 128), ("ni16", 128), ("hi16", 128), ("nh16", 128), ("sh16", 128), ("bo16", 128), ("nb16", 128), ("one16", 512), ("r0k", 128), ("prow", 128), ("imr", 128), ("c8k", 128),
          ("ksr", 128), ("cf", 48), ("v160", 256), ("v161", 256), ("elh", 16), ("jh", 256), ("nh", 256), ("jr", 16), ("eB", 256), ("IB", 256), ("lo", 512),
          ("oh", 256), ("pj", 256)),
    BF: (("idb", 128), ("nib", 128), ("k1b", 128), ("oneb", 128), ("wd", 128), ("bo4", 128), ("rcnt", 128), ("ze", 256), ("cm0", 128), ("cm1", 128), ("cn", 256),
         ("recb", 16), ("rB", 256), ("mk", 256)),
    I32: (("kx", 256), ("km0", 128), ("km1", 128), ("ui", 32), ("sq", 16), ("cmb0", 48), ("cmb1", 48), ("bs", 16), ("ei", 256), ("ej", 256), ("vi", 256), ("vj", 256), ("ki", 64), ("el", 16), ("kj", 32)),
    U16: (("e16", 256), ("elu", 16), ("ju", 256), ("nu", 256), ("of", 64), ("ILu", 16)),
}
PLACE = {}
for _d, _a in ((F32, "fA"), (F16, "hA"), (BF, "bA"), (I32, "iA"), (U16, "uA")):
    _at = 0
    for _n, _w in _SMALL[_d]:
        PLACE[_n] = (_a, _at, _w)
        _at += -(-_w // 32) * 32
    SCRATCH[_a] = ("sbuf", [128, _at], _d)
for _k in range(8):
    SCRATCH["ps%d" % _k] = ("psum", [128, 512], F32)
NDMA = 20
SEMAPHORES = ["eV", "eS", "eP", "eG", "snd", "arr1", "arr2", "arr3"] + ["d%d" % k for k in range(NDMA)]

CY = 0.00083 * 1.15
GA, SC, PEC, VO, WAKE = 1.4, 3.0, 0.0005, 0.03, 0.06


def rank_program(g, core, T, topo):
    rank = T.rank_of(core)
    if rank is None:
        return
    ops, hist, head = [], {}, [0.0]
    queues = {"V": g.vector, "S": g.scalar, "P": g.tensor, "G": g, "Y": g.sync}

    def A(name, lo=0, hi=None, step=1):
        if name in PLACE:
            name, at, w = PLACE[name]
            lo, hi = at + lo, at + (w if hi is None else hi)
        hi = T[name].shape[1] if hi is None else hi
        return (T[name][:, lo:hi] if step == 1 else T[name][:, lo:hi:step], (name, lo, hi, step))

    def meets(a, b):
        if a[1] >= b[2] or b[1] >= a[2]:
            return False
        return not (a[3] == b[3] and a[3] > 1 and a[1] % a[3] != b[1] % b[3])

    def add(q, calls, w, r, cost, lat=0.0, kind="c", sem=None, val=1):
        o = {"q": q, "calls": calls, "cost": cost, "lat": lat, "kind": kind, "sem": sem, "val": val, "deps": {}, "i": len(ops), "head": head[0]}
        for regs, isw in ((r, False), (w, True)):
            for reg in regs:
                ps = reg[0][:2] == "ps"
                for (p, preg, pw) in hist.setdefault(reg[0], []):
                    same = p["q"] == q and p["kind"] == "c" and kind == "c"
                    if ps and not same:
                        o["deps"][p["i"]] = True
                    elif meets(reg, preg) and (isw or pw):
                        need = not (same and q == "P")
                        o["deps"][p["i"]] = o["deps"].get(p["i"], False) or need
        for regs, isw in ((r, False), (w, True)):
            for reg in regs:
                h = hist[reg[0]]
                if isw and reg[3] == 1 and reg[0][:2] != "ps":
                    h[:] = [x for x in h if not (x[0] is not o and x[1][1] >= reg[1] and x[1][2] <= reg[2])]
                h.append((o, reg, isw))
        ops.append(o)

    def vcost(n, f=1.0):
        return VO + max(64.0, n * f) * CY

    def width(x):
        return (x[1][2] - x[1][1] + x[1][3] - 1) // x[1][3]

    def fast(*xs):
        return 0.5 if all(SCRATCH[x[1][0]][2] in (BF, F16, U16) for x in xs) else 1.0

    def cp(o, i):
        add("V", [lambda: g.vector.tensor_copy(o[0], i[0])], [o[1]], [i[1]], vcost(width(i), fast(o, i)))

    def tt(o, a, b, op):
        f = 1.0 if a[1][0][:2] == "ps" or b[1][0][:2] == "ps" else 2.0
        add("V", [lambda: g.vector.tensor_tensor(o[0], a[0], b[0], op)], [o[1]], [a[1], b[1]], vcost(width(a), f))

    def ts(o, a, s1, op0, s2=None, op1=None):
        r = [a[1]] + [s[1] for s in (s1, s2) if isinstance(s, tuple)]
        x1 = s1[0] if isinstance(s1, tuple) else s1
        x2 = s2[0] if isinstance(s2, tuple) else s2
        if op1 is None:
            f = lambda: g.vector.tensor_scalar(o[0], a[0], x1, None, op0)
        else:
            f = lambda: g.vector.tensor_scalar(o[0], a[0], x1, x2, op0, op1)
        add("V", [f], [o[1]], r, vcost(width(a), fast(o, a)))

    def ms(o, v):
        add("V", [lambda: g.vector.memset(o[0], v)], [o[1]], [], vcost(width(o), fast(o)))

    def scan(o, d0, d1, init, op0, op1):
        add("V", [lambda: g.vector.tensor_tensor_scan(o[0], d0[0], d1[0], init, op0, op1)], [o[1]], [d0[1], d1[1]], vcost(width(d1), fast(o, d0, d1)))

    def total_of(o, i):
        add("V", [lambda: g.vector.tensor_reduce(o[0], i[0], AX.X, OP.add)], [o[1]], [i[1]], vcost(width(i)))

    def act(o, i, func, scale=1.0, bias=0.0):
        r = [i[1]] + ([scale[1]] if isinstance(scale, tuple) else [])
        sc = scale[0] if isinstance(scale, tuple) else scale
        add("S", [lambda: g.scalar.activation(o[0], i[0], func, bias, sc)], [o[1]], r, 0.07 + width(i) * CY)

    def gat(q, o, win, off, scale=1.0):
        if q == "V":
            f = lambda: g.vector.tensor_copy(o[0], win[0].indirect(off[0]))
        else:
            f = lambda: g.scalar.activation(o[0], win[0].indirect(off[0]), AF.Copy, 0.0, scale)
        add(q, [f], [o[1]], [win[1], off[1]], 0.07 + 16 * width(off) * GA * CY)

    def gatop(o, win, off, b, op):
        add("V", [lambda: g.vector.tensor_tensor(o[0], win[0].indirect(off[0]), b[0], op)], [o[1]], [win[1], off[1], b[1]], 0.07 + 16 * width(off) * GA * CY)

    def pe(out, terms, first=True, last=True):
        calls, regs, n, c = [], [], len(terms), 0.05
        for k, (po, l, r) in enumerate(terms):
            calls.append(lambda po=po, l=l, r=r, k=k: g.tensor.matmul(po[0], l[0], r[0], first and k == 0, last and k == n - 1))
            regs += [l[1], r[1]]
            c += max(64, width(po)) * PEC
        add("P", calls, [out[1]], sorted(set(regs)), c)

    def spread(out_name, lo, src):
        calls, regs = [], [src[1]]
        w = 16 * width(src)
        for rho in range(16):
            po = A(out_name, lo + rho, lo + w, 16)
            l = A("R", rho * 128, rho * 128 + 128)
            calls.append(lambda po=po, l=l: g.tensor.matmul(po[0], l[0], src[0], True, True))
            regs.append(l[1])
        add("P", calls, [(out_name, lo, lo + w, 1)], regs, 0.05 + 16 * 64 * PEC)

    def collect(out, src, lo):
        pe(out, [(out, A("SF", rho * 128, rho * 128 + 128), A(src, lo + rho, lo + 256, 16)) for rho in range(16)])

    dn = [0]

    def dma(q, o, i, lat, regs_w, regs_r, acc=False):
        sem = "d%d" % dn[0]
        dn[0] += 1
        if acc:
            f = lambda: g.dma_start(o, i, accum_op=OP.add, max_dma_last_dim=4096)
        else:
            f = lambda: queues[q].dma_start(o, i)
        add(q, [f], regs_w, regs_r, 1.0 if q == "G" else 0.1, lat, "d", sem, 16)

    def load(q, name, src, lat, hi=None):
        a = A(name, 0, hi)
        dma(q, a[0], T[src][:], lat, [a[1]], [])

    load("Y", "hki", "hk", 2.2)
    load("S", "wti", "wt", 2.2)
    load("Y", "zin0", "zc", 2.4)
    load("S", "thi", "th", 2.4)
    load("Y", "gist", "gi", 4.0, E)
    load("Y", "ixi", "ix", 6.0)
    load("Y", "lki", "lk", 7.0)
    load("Y", "xcb", "xc", 8.0)

    def aff(o, i, pat, op, base, cm, fill=0.0):
        add("G", [lambda: g.affine_select(o[0], i[0], pat, op, fill, base, cm)], [o[1]], [i[1]], 0.2 + 2 * width(i) * CY)

    def gcp(o, i):
        add("G", [lambda: g.affine_select(o[0], i[0], [[1, width(o)]], OP.is_ge, 0.0, 1, 0)], [o[1]], [i[1]], 0.2 + 2 * width(o) * CY)

    def iot(o, pat, base, cm):
        add("G", [lambda: g.iota(o[0], pat, base, cm, allow_small_or_imprecise_dtypes=True)], [o[1]], [], 0.16 + 2 * width(o) * CY)

    def rep(name, n, w, cp=cp):
        k = w
        while k < n:
            cp(A(name, k, 2 * k), A(name, 0, k))
            k *= 2

    head[0] = 80.0
    ms(A("one"), 1.0)
    head[0] = 70.0
    ms(A("one16"), 1.0)
    ms(A("SW"), 0.0)
    head[0] = 0.0
    for k in range(0, 2048, 512):
        ms(A("S", k, k + 512), 0.0)
    head[0] = 60.0
    aff(A("blk"), A("one"), [[-16, 8], [0, 16]], OP.is_ge, 0, 1)
    aff(A("blk"), A("blk"), [[16, 8], [0, 16]], OP.is_ge, 15, -1)
    aff(A("idf"), A("one"), [[-1, 128]], OP.is_equal, 0, 1)
    tt(A("pm64"), A("idf", 0, 64), A("idf", 64, 128), OP.add)
    tt(A("pm32"), A("pm64", 0, 32), A("pm64", 32, 64), OP.add)
    tt(A("pm"), A("pm32", 0, 16), A("pm32", 16, 32), OP.add)
    cp(A("wtf"), A("wti"))
    ts(A("wblk"), A("blk"), A("wtf"), OP.mult)
    for k in range(0, 16, 2):
        cp(A("SW", k * 129, k * 128 + 128, 16), A("wblk", 0, 128, 16))
        act(A("SW", k * 129 + 129, k * 128 + 256, 16), A("blk", 0, 128, 16), AF.Copy, A("wtf"))
    head[0] = 0.0
    for k in range(16):
        act(A("S", k * 129, k * 128 + 128, 16), A("blk", 0, 128, 16), AF.Copy)
    cp(A("hkf"), A("hki"))
    cp(A("thf"), A("thi"))
    head[0] = 60.0
    for k in range(0, 16, 4):
        aff(A("R", k * 128, k * 128 + 512), A("one16"), [[-1, 4], [-16, 8], [0, 16]], OP.is_equal, -k, 1)
    head[0] = 0.0
    iot(A("im"), [[1, 16]], 0, 0)
    ts(A("pd", 0, 16), A("pm"), A("hkf", 0, 1), OP.mult)
    ts(A("pd", 16, 32), A("pm"), A("thf", 0, 1), OP.mult)
    pe(A("ps5", 64, 96), [(A("ps5", 64, 96), A("blk"), A("pd"))])
    cp(A("prow", 0, 16), A("ps5", 64, 80))
    rep("prow", 128, 16)
    cp(A("imr", 0, 16), A("im"))
    rep("imr", 128, 16)
    ms(A("c8k"), -8192.0)
    ts(A("r0k"), A("R", 0, 128), 2048.0, OP.mult)
    ms(A("rmin"), -4.0e7)
    ms(A("rmin", 0, 128, 16), 4.0e7)
    ms(A("zer"), 0.0)
    for name, c, off in (("idb", 1.0, 0), ("nib", -1.0, 0), ("id16", 1.0, 0), ("ni16", -1.0, 0), ("hi16", 0.5, 0), ("nh16", -0.5, 0), ("k1b", 1024.0, 0), ("sh16", 1.0, -1)):
        aff(A(name), A("zer"), [[-1, 128]], OP.not_equal, off, 1, c)
    aff(A("D"), A("R"), [[1, 16], [0, 8], [-1, 16]], OP.is_equal, 0, 0)
    ms(A("nx0", 2048, 2064), 0.0)
    ms(A("nx1", 2048, 2064), 0.0)
    for k in range(0, 2048, 512):
        ms(A("rz", k, k + 512), -100.0)
        ms(A("rz", k, k + 512, 16), 100.0)
    ms(A("half"), 0.5)
    ms(A("zero"), 0.0)
    scan(A("pw"), A("half"), A("zero"), 2.0, OP.mult, OP.add)
    tt(A("tw"), A("pw"), A("pm"), OP.mult)
    total_of(A("wcol"), A("tw"))
    tt(A("tr"), A("im"), A("pm"), OP.mult)
    total_of(A("rcol"), A("tr"))
    act(A("wd"), A("blk"), AF.Copy, A("wcol"))
    act(A("bo4"), A("blk"), AF.Copy, 4.0)
    ts(A("thr", 0, 16), A("pw"), 2.0, OP.mult)
    rep("thr", 256, 16, gcp)
    iot(A("lan0"), [[16, 16]], E, 0)
    ts(A("lane", 0, 16), A("lan0"), A("rcol"), OP.add)
    ts(A("lane", 16, 32), A("lane", 0, 16), float(E - W), OP.subtract)
    ts(A("kcol"), A("rcol"), -1.0, OP.mult, 15.0, OP.add)
    for k in range(0, 2048, 512):
        gcp(A("SF", k, k + 512), A("S", k, k + 512))
    if "V" in FPLAN:
        for k in range(0, 2048, 1024):
            act(A("NS", k, k + 1024), A("S", k, k + 1024), AF.Copy, -1.0)
    ts(A("ksr", 0, 16), A("im"), -1.0, OP.mult, 15.0, OP.add)
    ts(A("akey", 0, 16), A("ps5", 80, 96), 16.0, OP.mult)
    tt(A("akey", 0, 16), A("akey", 0, 16), A("ksr", 0, 16), OP.add)
    ms(A("ksr", 15, 16), -32768.0)
    ms(A("akey", 15, 16), -1.0e6)
    rep("ksr", 128, 16, gcp)
    rep("akey", 128, 16, gcp)
    ms(A("rmax"), 4.0e7)
    ms(A("rmax", 0, 128, 16), -4.0e7)
    ms(A("rcnt"), 1.0)
    ms(A("rcnt", 0, 128, 16), 0.0)
    ms(A("oneb"), 1.0)
    gcp(A("bo16"), A("blk"))
    ts(A("thf", 1, 2), A("thf", 1, 2), -1.0, OP.mult, -0.5, OP.add)
    ts(A("nb16"), A("idf"), A("thf", 1, 2), OP.mult)

    def quad(name, c0, c1):
        return (T[name][:, c0:c1, :, :], (name, c0 * 256, c1 * 256, 1))

    def line(name, rho):
        return (T[name][:, :, rho, :], (name, 0, 2048, 1))

    bank = [0]

    def plan(s):
        return [(q, 64 * k, 64) for k, q in enumerate(s)]

    def absdiff(parts, win, off, raw, other, sub, dest, scale):
        for (q, l0, n) in parts:
            h, a, b = l0 // 128, (l0 % 128) * 16, (l0 % 128 + n) * 16
            head[0] = HEAD * (1 - h)
            o = A("%s%d" % (raw, h), a, b)
            if q == "V":
                gatop(o, win, A(off, l0, l0 + n), other(h, a, b), OP.subtract if sub else OP.add)
                for x in range(a, b, 1024):
                    act(quad("%s%d" % (dest, h), x // 256, min(x + 1024, b) // 256), A("%s%d" % (raw, h), x, min(x + 1024, b)), AF.Abs, scale)
            else:
                gat("S", o, win, A(off, l0, l0 + n))
                for x in range(a, b, 512):
                    y = min(x + 512, b)
                    ps = A("ps%d" % bank[0], 0, y - x)
                    bank[0] ^= 1
                    pe(ps, [(ps, A("idb"), A("%s%d" % (raw, h), x, y)), (ps, A("nib" if sub else "idb"), other(h, x, y))])
                    act(quad("%s%d" % (dest, h), x // 256, y // 256), ps, AF.Abs, scale)

    def firsts(bc, own, eqn, lo_lo, small, extra=None):
        bank7 = (None, ("ps7", 0, 512, 1))
        O = lambda x, y: A("ps7", 256 + x, 256 + y)
        E3 = lambda c, x, y: (T[eqn][:, c, x:y], (eqn, 256 * c + x, 256 * c + y, 1))
        if extra:
            pe(bank7, [(O(0, 256),) + extra], True, False)
        else:
            rest = []
        for c0, c1 in ((0, 3), (3, 7), (7, 11), (11, 16)):
            calls, w, r, cost = [], [], [], 0.0
            for c in range(c0, c1):
                o = E3(c, 0, 256 - 16 * c)
                i = A(bc, 16 * c, 256)
                s = A(own, c, c + 1)
                calls.append(lambda o=o, i=i, s=s: g.vector.tensor_scalar(o[0], i[0], s[0], None, OP.is_equal))
                w.append(o[1])
                r += [i[1], s[1]]
                cost += vcost(256 - 16 * c, 0.5)
            add("V", calls, w, sorted(set(r)), cost)
            terms = [(O(16 * c + 16, 256), A("bo4"), E3(c, 16, 256 - 16 * c)) for c in range(c0, min(c1, 15))]
            if extra:
                pe(bank7, terms, False, False)
            else:
                rest += terms
        own_block = (O(0, 256), A("wd"), (T[eqn][:, :, 0:16], (eqn, 0, 4096, 1)))
        if extra:
            pe(bank7, [own_block], False, True)
        else:
            pe(bank7, [own_block] + rest)
        tt(A("lo", lo_lo, lo_lo + 256), O(0, 256), A("thr"), OP.is_ge)
        collect(A("ps5", small, small + 16), "lo", lo_lo)

    def sel(k, own, t, dlt):
        tt(A("dT", 16 * k, 16 * k + 16), t, dlt, OP.mult)
        tt(A("oT", 16 * k, 16 * k + 16), A("dT", 16 * k, 16 * k + 16), own, OP.add)
        cp(A("of", 16 * k, 16 * k + 16), A("oT", 16 * k, 16 * k + 16))

    def scat(win, off, src, src2=None):
        if src2 is None:
            f = lambda: g.vector.tensor_copy(win[0].indirect(off[0]), src[0])
        else:
            f = lambda: g.vector.tensor_tensor(win[0].indirect(off[0]), src[0], src2[0], OP.add)
        add("V", [f], [win[1]], [off[1], src[1]] + ([src2[1]] if src2 else []), 0.06 + 256 * SC * CY)

    def cues(t):
        head[0] = HC
        z, cb, v16 = "zin%d" % t, "cmb%d" % (t & 1), "v16%d" % (t & 1)
        u = A("ps6", 0, 16)
        pe(u, [(u, A("SW", r * 128, r * 128 + 128), A(z, r, 256, 16)) for r in range(16)])
        cp(A("ui", 0, 16), u)
        ts(A("ui", 16, 32), A("ui", 0, 16), 4095, OP.bitwise_and)
        tt(A("sq"), A("ui", 16, 32), A("ui", 16, 32), OP.mult)
        ts(A(cb, 0, 16), A("ui", 0, 16), 2047, OP.bitwise_and)
        ts(A(cb, 16, 32), A("sq"), 5, OP.logical_shift_right, 2047, OP.bitwise_and)
        ts(A(cb, 32, 48), A("sq"), 4, OP.logical_shift_right, 1023, OP.bitwise_and)
        cp(A("cf"), A(cb))
        spread("ps6", 0, A("cf", 0, 32))
        act(A("xe"), A("ps6", 0, 256), AF.Copy, A("hkf", 0, 1))
        act(A("xq"), A("ps6", 0, 256), AF.Copy, A("hkf", 1, 2))
        tt(A("ei" if t == 0 else "e0"), A("ps6", 256, 512), A("xe"), OP.add)
        spread("ps6", 0, A("cf", 32, 48))
        tt(A("vi"), A("ps6", 0, 256), A("xq"), OP.add)
        ts(A("vj"), A("vi"), 1023, OP.bitwise_and)
        gcp(A(v16), A("vj"))
        zr = "zr%d" % (t & 1)
        head[0] = 0.0
        for k in range(0, 16, 4):
            if ZPLAN[t][k // 4] == "S":
                add("S", [lambda m=m: g.scalar.activation(T[zr][:, m::16], T[z][:], AF.Copy, 0.0, 1.0) for m in range(k, k + 4)],
                    [(zr, m, 4096, 16) for m in range(k, k + 4)], [(z, 0, 256, 1)], 4 * (0.07 + 256 * CY))
            elif ZPLAN[t][k // 4] == "G":
                for m in range(k, k + 4):
                    gcp(A(zr, m, 4096, 16), A(z))
            else:
                add("V", [lambda m=m: g.vector.tensor_copy(T[zr][:, m::16], T[z][:]) for m in range(k, k + 4)],
                    [(zr, m, 4096, 16) for m in range(k, k + 4)], [(z, 0, 256, 1)], 4 * vcost(256, 0.5))

    cues(0)
    H = ((0, 0, 128), (1, 128, 256))
    for t in range(RO):
        z, zr, cb = "zin%d" % t, "zr%d" % (t & 1), "cmb%d" % (t & 1)
        for (h, a, b) in H:
            if t:
                ts(A("ei", a, b), A("e0", a, b), A("acol"), OP.add)
            ts(A("ej", a, b), A("ei", a, b), 2047, OP.bitwise_and)
            cp(A("e16", a, b), A("ej", a, b))
        if t:
            ts(A("bs"), A(cb, 16, 32), A("acol"), OP.add)
        base, boff = ("bs", 0) if t else (cb, 16)
        absdiff(plan(GPLAN[t]), A("gist", 0, E), "e16", "gd", lambda h, x, y: A(zr, h * 2048 + x, h * 2048 + y), True, "aa", 32768.0)
        for (h, a, b) in H:
            head[0] = HEAD * (1 - h)
            c0, c1 = 8 * h, 8 * h + 8
            k = A("ps%d" % (2 + h), 0, 128)
            pe(k, [(k, A("R", 0, 128), A("prow")), (k, A("r0k"), A("imr")), (k, A("r0k"), A("c8k"))]
               + [(k, A("S", r * 128, r * 128 + 128), line("aa%d" % h, r)) for r in range(16)])
            scan(A("km%d" % h), A("rmin"), k, 4.0e7, OP.max, OP.min)
            i0, i1, i2, i3 = [A("ki", 32 * h + 8 * x, 32 * h + 8 * x + 8) for x in range(4)]
            ts(i1, A("km%d" % h, 15, 128, 16), 2047, OP.bitwise_and)
            tt(i2, i1, A(cb, c0, c1), OP.mult)
            tt(i3, i2, A(base, boff + c0, boff + c1), OP.add)
            ts(A("el", c0, c1), i3, 2047, OP.bitwise_and)
            cp(A("elu", c0, c1), A("el", c0, c1))
            gat("V", A("ju", a, b), A("nm", 0, E) if t else A("ixi"), A("elu", c0, c1))
            for q in (0, 64):
                gat("V", A("lg%d" % h, 16 * q, 16 * q + 1024), A("lkt", 0, W) if t else A("lki"), A("ju", a + q, a + q + 64))
                gat("S", A("nx%d" % h, 16 * q, 16 * q + 1024), A("xcb"), A("ju", a + q, a + q + 64), -1.0)
                n = A("ps%d" % (2 + h), 128 + q, 192 + q)
                pe(n, [(n, A("D", r * 128, r * 128 + 128), A("lg%d" % h, 16 * q + r, 16 * q + 1024, 16)) for r in range(16)])
                cp(A("nu", a + q, a + q + 64), n)
            gcp(A("jh", a, b), A("ju", a, b))
            gcp(A("nh", a, b), A("nu", a, b))
            head[0] = HZ
            scan(A("zs%d" % h), A("rz"), A("nx%d" % h, 0, 2048), 100.0, OP.max, OP.min)
            zp = A("ps6", a, b)
            pe(zp, [(zp, A("idb"), A(z, a, b)), (zp, A("nib"), A("zs%d" % h, 15, 2048, 16))])
            act(A("ze", a, b), zp, AF.Copy, 0.5, 127.75)
            act(A("zo%d" % t, a, b), A("ze", a, b), AF.Copy, 1.0, -128.0)
        dst = T.cores[(rank + 1) % len(T.cores)] if t < RO - 1 else T.cores[(rank - t) % len(T.cores)]
        land = "zin%d" % (t + 1) if t < RO - 1 else "zfin"
        eng = topo.engines(core, dst)[:NENG]
        rid, pid, _se = topo.addr(dst)
        mask = sum(1 << e for e in eng)
        add("G", [lambda land=land, rid=rid, pid=pid, mask=mask, t=t: g.remote_dma(
            T[land][:], T["zo%d" % t][:], T.sem["arr%d" % (t + 1)], T.sem.snd, pid, rid, mask)],
            [(land, 0, 256, 1)], [("zo%d" % t, 0, 256, 1)], 1.0, 3.0, "r", "arr%d" % (t + 1), len(eng))
        head[0] = 0.0
        for (h, a, b) in H:
            x = A(zr, h * 2048, h * 2048 + 2048)
            dma("G", x[0], T["nx%d" % h][:, 0:2048], 5.0, [x[1]], [x[1], ("nx%d" % h, 0, 2048, 1)], acc=True)
        gcp(A("elh"), A("el"))
        gcp(A("elf"), A("el"))
        tt(A("dE", 0, 16), A("lane", 0, 16), A("elf"), OP.subtract)
        spread("ps7", 0, A("elh"))
        cp(A("eB"), A("ps7", 0, 256))
        firsts("eB", "elf", "eq", 0, 32)
        ts(A("loL"), A("ps5", 32, 48), 0.0625, OP.mult)
        sel(0, A("elf"), A("loL", 0, 16), A("dE", 0, 16))
        for (h, a, b) in H:
            c0, c1 = 8 * h, 8 * h + 8
            absdiff([p for p in plan(YPLAN[t]) if p[1] // 128 == h], A("xcb"), "nu", "yb", lambda h, x, y: A("nx%d" % h, x + 1, y + 1), False, "ya", 16.0)
            k = A("ps%d" % (2 + h), 256, 384)
            pe(k, [(k, A("R", 0, 128), A("ksr"))] + [(k, A("S", r * 128, r * 128 + 128), line("ya%d" % h, r)) for r in range(16)])
            tt(A("cm%d" % h), k, A("akey"), OP.is_le)
            scan(A("cn", a, b), A("rcnt"), A("cm%d" % h), 0.0, OP.mult, OP.add)
            scan(A("kx", a, b), A("rmax"), k, -4.0e7, OP.min, OP.max)
        ts(A("rec"), A("cn", 15, 256, 16), float(NEED), OP.is_ge)
        cp(A("recb"), A("rec"))
        ts(A("kj", 16, 32), A("kx", 15, 256, 16), 15, OP.bitwise_and)
        head[0] = 0.0
        if t < RO - 1:
            cues(t + 1)
            cnt = A("ps3", 384, 400)
            pe(cnt, [(cnt, A("oneb"), A("recb"))])
            total_of(A("acol"), cnt)
            ts(A("nrec"), A("rec"), -1.0, OP.mult, 1.0, OP.add)
            tt(A("gT"), A("loL", 0, 16), A("nrec"), OP.max)
            sel(1, A("elf"), A("gT"), A("dE", 0, 16))
            scat(A("gist"), A("of", 16, 32), A(z))
        F = A("ps4", 0, 256)
        jp = A("ps4", 256, 512)
        pe(jp, [(jp, A("id16"), A("jh"))])
        pe((None, ("ps4", 0, 512, 1)), [(F, A("nb16"), A("one16", 0, 256))], True, False)
        for (h, a, b) in H:
            fh = A("ps4", a, b)
            terms = [(fh, A("S", r * 128, r * 128 + 128), A("fa%d" % h, r, 2048, 16)) for r in range(16)]
            if FPLAN[h] == "S":
                for x in (0, 1024):
                    act(A("fa%d" % h, x, x + 1024), A(zr, h * 2048 + x, h * 2048 + x + 1024), AF.Abs)
            else:
                for x in (0, 1024):
                    ts(A("fa%d" % h, x, x + 1024), A(zr, h * 2048 + x, h * 2048 + x + 1024), 0.0, OP.max, 2.0, OP.mult)
                terms += [(fh, A("NS", r * 128, r * 128 + 128), A(zr, h * 2048 + r, h * 2048 + 2048, 16)) for r in range(16)]
            pe(fh, terms, False, False)
        ts(A("rec"), A("rec"), 16.0, OP.mult)
        tt(A("jr"), A("kj", 16, 32), A("rec"), OP.add)
        spread("ps5", 256, A("jr"))
        act(A("rB"), A("ps5", 256, 512), AF.Relu, 1.0, -15.0)
        ts(A("oh"), A("ps5", 256, 512), A("kcol"), OP.is_equal)
        tt(A("pj"), A("ps4", 256, 512), A("oh"), OP.mult)
        pe(F, [(F, A("k1b"), A("rB"))], False, True)
        dp, ib = A("ps6", 0, 256), A("ps6", 256, 512)
        pe(ib, [(ib, A("bo16"), A("pj")), (ib, A("k1b"), A("rB"))])
        cp(A("IB"), ib)
        pe(dp, [(dp, A("sh16"), A("jh")), (dp, A("ni16"), A("nh"))])
        tt(A("dl"), dp, A("oh"), OP.mult)
        v = A("v16%d" % (t & 1))
        hp, hm = A("ps6", 0, 256), A("ps6", 256, 512)
        pe(hp, [(hp, A("hi16"), v), (hp, A("hi16"), A("jh"))])
        act(A("ja"), hp, AF.Copy)
        pe(hm, [(hm, A("hi16"), v), (hm, A("nh16"), A("jh"))])
        act(A("mk"), F, AF.Sign)
        tt(A("pn"), hm, A("mk"), OP.mult)
        if t == 0:
            for x in range(0, E, 512):
                gcp(A("nm", x, x + 512), A("ixi", x, x + 512))
            for x in range(0, W, 512):
                gcp(A("lkt", x, x + 512), A("lki", x, x + 512))
        scat(A("nm"), A("of", 0, 16), A("pn"), A("ja"))
        collect(A("ps5", 48, 64), "pj", 0)
        cp(A("ILu"), A("ps5", 48, 64))
        ts(A("dT", 48, 64), A("rec"), 128.0, OP.mult)
        tt(A("IL"), A("ps5", 48, 64), A("dT", 48, 64), OP.add)
        gatop(A("nl"), A("lkt", 0, W), A("ILu"), A("dl"), OP.add)
        tt(A("dE", 16, 32), A("lane", 16, 32), A("IL"), OP.subtract)
        ts(A("dE", 16, 32), A("dE", 16, 32), 0.0625, OP.mult)
        firsts("IB", "IL", "eq2", 256, 96, (A("k1b"), A("rB")))
        sel(2, A("IL"), A("ps5", 96, 112), A("dE", 16, 32))
        scat(A("lkt"), A("of", 32, 48), A("nl"))
    dma("Y", T.yz[:], T.zfin[:], 2.5, [], [("zfin", 0, 256, 1)])
    dma("Y", T.yi[:], T.nm[:, 0:E], 5.0, [], [("nm", 0, E, 1)])
    dma("Y", T.yl[:], T.lkt[:, 0:W], 3.5, [], [("lkt", 0, W, 1)])

    n = len(ops)
    users = [[] for _ in range(n)]
    for o in ops:
        for d in o["deps"]:
            users[d].append(o["i"])
    way = [0.0] * n
    for i in range(n - 1, -1, -1):
        o = ops[i]
        way[i] = o["cost"] + o["lat"] + max([way[j] + WAKE for j in users[i]] + [0.0])
    queue, cost = [o["q"] for o in ops], [o["cost"] for o in ops]
    tail = [o["cost"] + o["lat"] for o in ops]
    then = [[(j, tail[i] + WAKE if ops[j]["deps"][i] else 1e-6) for j in users[i]] for i in range(n)]
    npre = [len(o["deps"]) for o in ops]

    def place(key):
        left, avail, start, order = list(npre), [0.0] * n, [0.0] * n, []
        free, ready = {q: 0.0 for q in queues}, {q: [] for q in queues}
        for i in range(n):
            if left[i] == 0:
                ready[queue[i]].append(i)
        while len(order) < n:
            m, q = 1e18, None
            for x in ready:
                if ready[x]:
                    y = max(free[x], min(avail[i] for i in ready[x]))
                    if y < m:
                        m, q = y, x
            i = max((j for j in ready[q] if avail[j] <= m + LOOK), key=lambda j: key[j])
            s = start[i] = max(avail[i], free[q])
            free[q] = s + cost[i]
            ready[q].remove(i)
            order.append(i)
            for j, w in then[i]:
                left[j] -= 1
                if s + w > avail[j]:
                    avail[j] = s + w
                if left[j] == 0:
                    ready[queue[j]].append(j)
        return start, order, max(start[i] + tail[i] for i in range(n))

    if n not in ORDER:
        key = [way[i] + ops[i]["head"] for i in range(n)]
        best = place(key)
        rng = np.random.RandomState(5)
        for k in range(TRIES):
            nk = [float(x) for x in np.array(key) + (rng.rand(n) < (0.02, 0.1, 0.4)[k % 3]) * rng.randn(n) * (0.5, 2.0, 6.0)[(k // 3) % 3]]
            new = place(nk)
            if new[2] <= best[2]:
                key, best = nk, new
        ORDER[n] = best
    start, order, _span = ORDER[n]
    fin = [start[i] + tail[i] for i in range(n)]

    know = {q: {} for q in queues}
    clock = [None] * n
    count = {q: 0 for q in queues}
    total = {}
    for i in order:
        o = ops[i]
        q = o["q"]
        k = know[q]
        for d in sorted(o["deps"]):
            if not o["deps"][d]:
                continue
            sem, val, ck = clock[d]
            if k.get(sem, 0) < val:
                queues[q].wait_ge(T.sem[sem], val)
                k[sem] = val
                for s2, v2 in ck.items():
                    if k.get(s2, 0) < v2:
                        k[s2] = v2
        ck = dict(k)
        inst = None
        for f in o["calls"]:
            inst = f()
        if o["kind"] == "c":
            count[q] += 1
            inst.then_inc(T.sem["e" + q], 1)
            clock[i] = ("e" + q, count[q], ck)
            total["e" + q] = count[q]
        elif o["kind"] == "d":
            inst.then_inc(T.sem[o["sem"]], 16)
            clock[i] = (o["sem"], 16, ck)
            total[o["sem"]] = 16
        else:
            clock[i] = (o["sem"], o["val"], {})
            total[o["sem"]] = o["val"]
            total["snd"] = total.get("snd", 0) + o["val"]
    for sem in sorted(total):
        if know["G"].get(sem, 0) < total[sem]:
            g.wait_ge(T.sem[sem], total[sem])
